import numpy as np, ml_dtypes
CORES = [35,38,43,46]
N = 4
BF = ml_dtypes.bfloat16
def gentries(a):
    return np.ascontiguousarray(a.reshape(8, 16, -1).transpose(0, 2, 1)).reshape(8, -1)
def gtable(e):
    e = np.asarray(e); return np.ascontiguousarray(e.reshape(8, -1, 16).transpose(0, 2, 1)).reshape(128, -1).astype(np.int32)
W, R, PG, V, H = 4096, 16, 256, 5, 1
K = PG * R
def parts(rng):
    x = rng.integers(0, 256, (N, 8, 16, W)); e = rng.integers(0, 256, (N, 8, 16, PG)); w = rng.integers(0, 16, (N, 8, 16))
    h = rng.choice(np.array([1000, 1300, 1600, 1900]), (N, 8, 1)) + rng.integers(-300, 301, (N, 8, 16))
    l = rng.integers(0, W, (N, 8, K)); share = np.repeat(rng.choice(np.array([0.0, 0.3, 0.6, 0.9]), (N, 8, PG)), R, axis=2)
    s = np.where(rng.random((N, 8, K)) < share, l, rng.integers(0, W, (N, 8, K)))
    c = rng.random((N, 8, K)); p = np.where(c < 0.3, s, np.where(c < 0.4, l, rng.integers(0, W, (N, 8, K))))
    return x, e, w, h, p, s, l, rng.integers(0, W, (N, 8, K))
def pack(x, e, w, h, p, s, l, q):
    r = {"xt": x.reshape(N, 128, W).astype(np.float32).astype(BF), "ed": e.reshape(N, 128, PG).astype(np.float32).astype(BF),
         "wt": np.ascontiguousarray(w.reshape(N, 128, 1)).astype(np.int32), "th": np.ascontiguousarray(h.reshape(N, 128, 1)).astype(np.int32)}
    for k, z in (("pl", p), ("sl", s), ("ll", l), ("ql", q)): r[k] = np.stack([gtable(a) for a in z])
    return r
def setup_inputs(rng):
    return pack(*parts(rng))
def setup_inputs_spread(rng):
    x, e, w, h, p, s, l, q = parts(rng)
    x = np.minimum((np.exp2(8 * rng.random((N, 8, 1, W))) * rng.random((N, 8, 16, W))).astype(np.int64), 255)
    e = np.minimum((np.exp2(8 * rng.random((N, 8, 1, PG))) * rng.random((N, 8, 16, PG))).astype(np.int64), 255)
    w = (16 * rng.random((N, 8, 16)) ** 3).astype(np.int64); h = np.minimum(np.exp2(12 * rng.random((N, 8, 16))).astype(np.int64) - 1, 4080)
    p, s, l, q = [(W * rng.random((N, 8, K)) ** 3).astype(np.int64) for z in range(4)]
    s = np.where(rng.random((N, 8, K)) < np.repeat(rng.random((N, 8, PG)), R, axis=2), l, s)
    return pack(x, e, w, h, p, s, l, q)
def setup_inputs_ends(rng):
    x = 255 * rng.integers(0, 2, (N, 8, 16, W)); e = 255 * rng.integers(0, 2, (N, 8, 16, PG)); w = 15 * rng.integers(0, 2, (N, 8, 16)); h = 4080 * rng.integers(0, 2, (N, 8, 16))
    kind = rng.integers(0, 3, (N, 8, 1)); kind[:, 7] = 0; kind[0, 0] = 0; kind[1, 1] = 1
    x[..., 0] = np.where(kind == 0, 0, np.where(kind == 1, 255, x[..., 0])); x[..., W - 1] = np.where(kind == 0, 255, np.where(kind == 1, 0, x[..., W - 1]))
    w[:, :, 5] = 0; w[:, 7] = 15; w[:, :, 2] = 15; w[:, :, 13] = 15
    h[:, :, 0] = 0; h[:, :, 15] = 0; h[:, :, 1] = 4080; h[:, :, 14] = 4080
    p, s, l, q = [np.where(rng.random((N, 8, K)) < 0.75, (W - 1) * rng.integers(0, 2, (N, 8, K)), rng.integers(0, W, (N, 8, K))) for z in range(4)]
    pv, sv, lv = [z.reshape(N, 8, PG, R) for z in (p, s, l)]; k = np.arange(R)
    for i in (0, 1, 2, 3, PG - 4, PG - 3, PG - 2, PG - 1):
        pv[:, :, i] = 0; sv[:, :, i] = W - 1; lv[:, :, i] = W - 1
    lv[:, :, [0, PG - 1]] = np.where(k % 4 == 1, 0, W - 1)
    lv[:, :, [1, PG - 2]] = np.where((k % 4 == 1) | (k == 2), 0, W - 1)
    lv[:, :, [3, PG - 4]] = 0
    e[..., [0, PG - 1]] = 0; e[:, :, 2, [0, PG - 1]] = 255; e[:, :, 13, [0, PG - 1]] = 18
    e[..., [2, PG - 3]] = 0; e[..., [3, PG - 4]] = 255
    return pack(x, e, w, h, p, s, l, q)
def setup_inputs_corners(rng):
    x, e, w, h, p, s, l, q = parts(rng)
    cnt = np.roll(np.array([31, 32, 0, 8 * PG, 33, 1, 8 * PG - 1, 64])[:N], int(rng.integers(0, N))); fl = np.zeros((N, 8 * PG), bool)
    for r in range(N): fl[r, rng.permutation(8 * PG)[:int(cnt[r])]] = True
    fr = np.repeat(fl.reshape(N, 8, PG), R, axis=2)
    lv = l.reshape(N, 8, PG, R); lv[:, :, [0, PG - 1]] = (W - 1) * rng.integers(0, 2, (N, 8, 2, R))
    far = (l + rng.integers(1, W, l.shape)) % W; half = np.repeat(rng.random((N, 8, PG)) < 0.5, R, axis=2)
    s = np.where(fr, far, l); p = np.where(fr | half, l, rng.integers(0, W, l.shape))
    for g in range(8):
        if g % 4 < 3: q[:, g] = (l, s, p)[g % 4][:, g]
    w[:, 0] = 0; w[:, 7] = 15; w[:, 4] = 15; w[:, 3] = 0; w[:, 3, 15] = 15; w[:, 5] = 0; w[:, 5, 0] = 1
    h = np.where(rng.random(h.shape) < 0.5, rng.choice(np.array([0, 1, 4079, 4080]), h.shape), h)
    e[..., [0, PG - 1]] = 0; e[:, :, 2, [0, PG - 1]] = 255; e[:, :, 13, [0, PG - 1]] = 18
    e[..., 1] = 255; e[..., PG - 2] = 0
    return pack(x, e, w, h, p, s, l, q)
def setup_inputs_alike(rng):
    x, e, w, h, p, s, l, q = parts(rng)
    step = rng.choice(np.array([1, 4, 8, 32]), (N, 8, 1, 1)); lane = rng.integers(0, 8, (N, 8, 16, 1))
    x = step * (rng.integers(0, 8, (N, 8, 1, W)) ^ lane); e = step * (rng.integers(0, 8, (N, 8, 1, PG)) ^ lane)
    h = step[..., 0] * rng.integers(20, 81, (N, 8, 16))
    return pack(x, e, w, h, p, s, l, q)
def setup_inputs_near(rng):
    x, e, w, h, p, s, l, q = parts(rng); n = np.arange(N); f = rng.integers(0, 16, N); k = np.arange(R)
    s[:, 0] = l[:, 0]; h[:, 0] = 0
    h[:, 7] = 4080; x[:, 7, :, :2] = 0; x[:, 7, :, W - 2:] = 255; x[n, 7, f, 1] = 1; x[n, 7, f, W - 2] = 254
    pv, sv, lv, qv = [z.reshape(N, 8, PG, R)[:, 7] for z in (p, s, l, q)]
    for z in (pv, sv, lv): z[:, PG - 1] = W - 1; z[:, PG - 3] = W - 1
    pv[:, PG - 1, R - 4:] = 0; sv[:, PG - 1, R - 4:] = 0; qv[:, PG - 1, R - 4:] = W - 2
    pv[:, PG - 2] = 0; sv[:, PG - 2] = W - 1; sv[:, PG - 2, 0] = W - 2; lv[:, PG - 2] = np.where(k % 4 == 1, 0, W - 1)
    e[:, 7, :, PG - 3] = 0; e[n, 7, f, PG - 3] = 1
    pv[:, PG - 4] = 1; sv[:, PG - 4] = 0; lv[:, PG - 4] = W - 1
    return pack(x, e, w, h, p, s, l, q)
def check_inputs(d):
    bad = []
    for k, hi in (("xt", 255), ("ed", 255), ("wt", 15), ("th", 4080), ("pl", W - 1), ("sl", W - 1), ("ll", W - 1), ("ql", W - 1)):
        v = np.asarray(d[k]).astype(np.float64)
        if not (np.min(v) >= 0 and np.max(v) <= hi): bad.append("range of " + k)
        elif np.any(v != np.floor(v)): bad.append("whole numbers of " + k)
    return bad
def dist(y, z):
    return np.add.reduce(np.abs(y - z), axis=1, dtype=np.int32)
def reference(xt, ed, wt, th, pl, sl, ll, ql):
    x = xt.astype(np.float32).astype(np.int16).reshape(N, 8, 16, W); e = ed.astype(np.float32).astype(np.int16).reshape(N, 8, 16, PG)
    w = wt.astype(np.int32).reshape(N, 8, 16, 1); h = th.astype(np.int32).reshape(N, 8, 16)[:, :, np.arange(K) % 16]
    p, s, l, q = [np.stack([gentries(a) for a in z]).astype(np.int64) for z in (pl, sl, ll, ql)]
    more = 37 * (np.arange(K) % R); A = np.zeros(N, np.int64)
    for t in range(V):
        new = np.zeros_like(l); failed = np.zeros((N, 8, PG), bool); m = np.zeros((N, 8, 16, PG), np.int16)
        for r in range(N):
            vp, vs, vl, vq = [np.take_along_axis(x[r], z[r][:, None, :], 2) for z in (p, s, l, q)]
            a = dist(vp, vs); b = dist(vs, vl); c = dist(vp, vl); d = dist(vq, vs); o = dist(vl, np.repeat(e[r], R, axis=2))
            failed[r] = 2 * np.sum((c - b).reshape(8, PG, R), axis=2) < np.sum(a.reshape(8, PG, R), axis=2)
            u = np.repeat(np.sum(w[r] * e[r], axis=1) & (W - 1), R, axis=1).astype(np.int64)
            change = ((l[r] * u >> 5) + l[r] + more + A[r]) & (W - 1)
            new[r] = np.where(np.repeat(failed[r], R, axis=1) & (c < b), p[r], np.where(d < b, q[r], np.where(o >= h[r], change, l[r])))
            m[r] = np.max(vl.reshape(8, 16, PG, R), axis=3)
        got = np.roll(m, N // 2, axis=0)
        e = np.where(failed[:, :, None, :], np.abs(e - got), (e + got) >> 1)
        A = np.sum(failed, axis=(1, 2)).astype(np.int64) & 31
        q = np.where(new != l, l, q); p, s, l = s, l, new
        if t < V - 1: p, s, l, q = [np.roll(z, H, axis=0) for z in (p, s, l, q)]
    out = [np.stack([gtable(a) for a in z]).astype(np.float32) for z in (p, s, l, q)]
    return {"yp": out[0], "ys": out[1], "yl": out[2], "yq": out[3], "ye": e.reshape(N, 128, PG).astype(np.float32).astype(BF)}

@@ -1,0 +1,552 @@
+import numpy as np
+from concourse.mybir import AluOpType as OP, ActivationFunctionType as AF
+
+V, H2 = 5, 2
+PCS = 2
+PE_NS, CY_NS, GATH = 0.4167, 0.83, 1.5
+MAGIC = 8388608.0
+
+SCRATCH, SEMAPHORES = {}, ["sT", "sV", "sS", "sG", "lsem"]
+
+
+def _buf(name, cols, dtype, where="sbuf"):
+    SCRATCH[name] = (where, [128, cols], dtype)
+
+
+for _n in ("d0", "d1", "d2", "bA0", "bA1", "bB", "bD", "bE"):
+    _buf(_n, 512, "float32", "psum")
+for _t in range(4):
+    _buf("x%d" % _t, 4096 + 16, "bfloat16")
+    _buf("thm%d" % _t, 640, "bfloat16")
+    _buf("wb%d" % _t, 128, "bfloat16")
+for _h in range(2):
+    for _n in ("sg", "lg", "da", "dd", "ra", "rd", "ab", "ac", "ao", "mx"):
+        _buf(_n + str(_h), 2048, "bfloat16")
+    for _n in ("fl", "fz", "gf"):
+        _buf(_n + str(_h), 128, "bfloat16")
+ITMP, FTMP = ("ui", "uj", "z", "zs", "y", "ch", "r1", "nw"), ("m3", "r3", "m1", "ne", "absd", "t2", "sc")
+_buf("itmp", len(ITMP) * 256, "int32")
+_buf("ftmp", len(FTMP) * 256, "float32")
+_buf("mo", V * 256, "bfloat16")
+_buf("mi", V * 256, "bfloat16")
+_buf("u16l", 7 * 256, "uint16")
+_buf("u16q", 5 * 256, "uint16")
+_buf("lst", 5 * 256, "float32")
+_buf("lh", 6 * 256, "float16")
+_buf("qst", 6 * 256, "float32")
+_buf("qh", 6 * 256, "float16")
+_buf("outs", 4 * 256, "float32")
+for _t in range(V + 1):
+    for _h in range(2):
+        _buf("e%d%d" % (_t, _h), 144, "bfloat16")
+        if _t < V:
+            _buf("eo%d%d" % (_t, _h), 144, "bfloat16")
+            SEMAPHORES.append("rm%d%d" % (_t, _h))
+            if _t:
+                SEMAPHORES.append("re%d%d" % (_t, _h))
+SEMAPHORES += ["rx1", "rx2", "rx3"]
+for _n in ("pl", "sl", "ll", "ql"):
+    _buf("i_" + _n, 256, "int32")
+    _buf("f_" + _n, 256, "float32")
+_buf("i_tw", 2, "int32")
+_buf("i_th", 2, "int32")
+_buf("ka", 128, "float16")
+_buf("k37", 128, "float32")
+_buf("acol", 2, "int32")
+_buf("one32", 128, "float32")
+_buf("i32", 128, "float32")
+_buf("i16", 128, "float16")
+_buf("n16", 128, "float16")
+for _n in ("one", "ib", "nib", "hib", "i1024", "im512", "bt", "b128"):
+    _buf(_n, 128, "bfloat16")
+_buf("msk", 2048 // PCS, "bfloat16")
+_buf("mskk", 2048 // PCS, "bfloat16")
+_buf("fun", 80, "bfloat16")
+_buf("rowb", 256, "bfloat16")
+_buf("rowlo", 512, "bfloat16")
+_buf("rowq", 128, "bfloat16")
+LOADS = ["sl", "xt", "pl", "th", "wt", "ll", "ql", "ed0", "ed1"]
+STORES = ["%s%d" % (_n, _h) for _n in ("yp", "ys", "yl", "yq", "ye") for _h in range(2)]
+SEMAPHORES += ["d_" + _n for _n in LOADS + STORES]
+
+
+class _Bank(dict):
+    pass
+
+
+def _plan(g, core, T, topo):
+    rank, N = T.rank_of(core), len(T.cores)
+    ops, last_w, readers, accs, banks, half = [], {}, {}, {}, {}, ["0"]
+
+    def op(q, cost, fns, r=(), w=(), a=(), b=(), sig=None, lat=0.0, after=()):
+        o = {"q": q, "c": cost, "f": fns, "d": {}, "sig": sig, "lat": lat, "i": len(ops), "n": (list(w) + list(a) + list(r) + ["?"])[0]}
+        for x in after:
+            o["d"][x["i"]] = 1
+        r, w, a, b = [[k + half[0] if k in ("A", "A1", "bA") else k for k in ks] for ks in (r, w, a, b)]
+        for k in r:
+            for x in [last_w.get(k)] + accs.get(k, []):
+                if x is not None:
+                    o["d"][x["i"]] = 1
+        for k in a:
+            if last_w.get(k) is not None:
+                o["d"][last_w[k]["i"]] = 1
+            for x in readers.get(k, []):
+                o["d"][x["i"]] = 1
+        for k in w:
+            for x in [last_w.get(k)] + accs.get(k, []) + readers.get(k, []):
+                if x is not None:
+                    o["d"][x["i"]] = 1
+        for k in r:
+            readers.setdefault(k, []).append(o)
+        for k in a:
+            accs.setdefault(k, []).append(o)
+        for k in w:
+            last_w[k], accs[k], readers[k] = o, [], []
+        for k in b:
+            bk = banks.setdefault(k, {"q": None, "cur": [], "prev": []})
+            if bk["q"] != q:
+                bk["q"], bk["prev"], bk["cur"] = q, bk["cur"], []
+            for x in bk["prev"]:
+                o["d"][x["i"]] = 1
+            bk["cur"].append(o)
+        o["d"].pop(o["i"], None)
+        ops.append(o)
+        return o
+
+    def vec(n, cyc=1.0):
+        return max(64.0, n * cyc) * CY_NS / 1000
+
+    def mm(fns, cyc, **kw):
+        return op("T", cyc * PE_NS / 1000, fns, **kw)
+
+    def MM(out, lhsT, rhs, start, stop):
+        return lambda: g.tensor.matmul(out, lhsT, rhs, start, stop)
+
+    def v(fn, n, cyc=1.0, **kw):
+        return op("V", vec(n, cyc), [fn], **kw)
+
+    def s(fn, n, **kw):
+        return op("S", vec(n), [fn], **kw)
+
+    def tt(out, a, b, o):
+        return lambda: g.vector.tensor_tensor(out, a, b, o)
+
+    def ts(out, a, s1, o1, s2=None, o2=None):
+        if o2 is None:
+            return lambda: g.vector.tensor_scalar(out, a, s1, None, o1)
+        return lambda: g.vector.tensor_scalar(out, a, s1, s2, o1, o2)
+
+    def cp(out, a):
+        return lambda: g.vector.tensor_copy(out, a)
+
+    def act(out, a, f, bias=0.0, scale=1.0):
+        return lambda: g.scalar.activation(out, a, f, bias=bias, scale=scale)
+
+    def load(name, out, in_, key):
+        return op("Y", 0.1, [lambda: g.sync.dma_start(out, in_)], w=[key], sig=("d_" + name, 16), lat=4.0 if name == "xt" else 2.2)
+
+    def send(name, out, in_, dst, eng, key, lat, rkey, after=(), n_in=None):
+        eng = [e for e in eng]
+        m = sum(1 << e for e in eng)
+        rid, pid, _ = topo.addr(dst)
+        so = op("G", 1.3, [lambda: g.remote_dma(out, in_, T.sem[name], T.sem["lsem"], pid, rid, m)], r=[key], sig=("send", len(eng)), after=after)
+        op("R", 0.0, [], w=[rkey], sig=(name, n_in or len(eng)), after=[so], lat=lat)
+        return so
+
+    def dst(k):
+        return T.cores[(rank + k) % N]
+
+    def cb(name, i, h, n=128):
+        c = i * 256 + h * 128
+        return T[name][:, c:c + n]
+
+    load("sl", T.i_sl[:], T.sl[:], "i_sl")
+    load("xt", T.x0[:, 0:4096], T.xt[:], "x0")
+    load("pl", T.i_pl[:], T.pl[:], "i_pl")
+    load("th", T.i_tw[:, 0:1], T.th[:], "i_th")
+    load("wt", T.i_tw[:, 1:2], T.wt[:], "i_wt")
+    load("ll", T.i_ll[:], T.ll[:], "i_ll")
+    load("ql", T.i_ql[:], T.ql[:], "i_ql")
+    load("ed0", T.e00[:, 0:128], T.ed[:, 0:128], "e00")
+    load("ed1", T.e01[:, 0:128], T.ed[:, 128:256], "e01")
+    ms = lambda ap, c: (lambda: g.vector.memset(ap, c))
+    v(ms(T.one32[:], 1.0), 128, w=["one32"])
+    v(ms(T.one[:], 1.0), 128, w=["one"])
+    gq = lambda fn, n, **kw: op("G", 0.2 + n * 2 * CY_NS / 1000, [fn], **kw)
+    gq(lambda: g.affine_select(T.i32[:], T.one32[:], [[-1, 128]], OP.is_equal, 0.0, 0, 1), 128, r=["one32"], w=["i32"])
+    gq(lambda: g.affine_select(T.bt[:], T.one[:], [[-16, 8], [0, 16]], OP.is_ge, 0.0, 0, 1), 128, r=["one"], w=["bt"])
+    gq(lambda: g.affine_select(T.b128[:], T.bt[:], [[16, 8], [0, 16]], OP.is_ge, 0.0, 15, -1), 128, r=["bt"], w=["b128"])
+    gq(lambda: g.iota(T.mskk[:], [[0, 128 // PCS], [1, 16]], 0, 0, allow_small_or_imprecise_dtypes=True), 2048 // PCS, w=["mskk"])
+    gq(lambda: g.iota(T.k37[:], [[0, 8], [37, 16]], 0, 0, allow_small_or_imprecise_dtypes=True), 128, w=["k37"])
+    for nm, c in (("ib", 1.0), ("nib", -1.0), ("hib", 0.5), ("i1024", 1024.0), ("im512", -512.0), ("i16", 1.0), ("n16", -1.0)):
+        if nm in ("i16", "n16"):
+            v(ts(T[nm][:], T.i32[:], c, OP.mult), 128, r=["i32"], w=[nm])
+        else:
+            s(act(T[nm][:], T.i32[:], AF.Copy, 0.0, c), 128, r=["i32"], w=[nm])
+    v(ts(T.msk[:], T.mskk[:], 0.0, OP.is_gt), 2048 // PCS, 0.5, r=["mskk"], w=["msk"])
+    SC = 32768.0
+    FUN = {"ab": (0, 24), "ac": (24, 40), "ra": (40, 48), "da": (48, 56), "rd": (56, 64), "dd": (64, 72), "ao": (72, 80)}
+    for i, c in enumerate((SC, SC, -2.0, -SC, 2.0, -2.0, 1.0, -2 * SC, SC, SC)):
+        s(act(T.fun[:, 8 * i:8 * i + 8], T.b128[:, 0::16], AF.Copy, 0.0, c), 8, r=["b128"], w=["fun%d" % i])
+    for nm, a, b, c in (("rowlo", 0, 256, -SC / 2), ("rowlo", 256, 384, 0.0), ("rowlo", 384, 512, SC / 2),
+                        ("rowb", 0, 128, 2048.0), ("rowb", 128, 256, -2048.0), ("rowq", 0, 128, -0.25)):
+        v(ms(T[nm][0:1, a:b], c), b - a, w=[nm + str(a)])
+    for h in range(H2):
+        v(ms(T["fz%d" % h][:], 0.0), 128, 0.5, w=["fz0%d" % h])
+    CK = ["rowlo0", "rowlo256", "rowlo384"]
+    CB_ = ["rowb0", "rowb128"]
+    FK = ["fun%d" % i for i in range(10)]
+    one_row = T.one[0:1, :]
+    v(ts(T.i_th[:, 0:1], T.i_tw[:, 0:1], 4, OP.arith_shift_right), 1, r=["i_th"], w=["thh"])
+    v(ts(T.i_th[:, 1:2], T.i_tw[:, 0:1], 15, OP.bitwise_and), 1, r=["i_th"], w=["thl"])
+    v(ms(T.x0[:, 4096:4112], 0.0), 16, w=["xe0"])
+    v(ts(T.x0[:, 4096:4097], T.i_th[:, 0:1], -SC * 16, OP.mult), 1, r=["thh"], w=["xe0"])
+    v(ts(T.x0[:, 4097:4098], T.i_th[:, 1:2], -SC, OP.mult), 1, r=["thl"], w=["xe0"])
+    v(cp(T.x0[:, 4098:4099], T.i_tw[:, 1:2]), 1, r=["i_wt"], w=["xe0"])
+    tab_ready = [o for o in ops if o["i"] in (last_w["x0"]["i"], last_w["xe0"]["i"])]
+
+    def send_table(t, after):
+        def tab_engines(a, b):
+            en = topo.engines(a, b)
+            return en[8:16] if len(en) >= 16 else (en[0:8] if t == 1 else en[0:4])
+
+        d = dst(-t)
+        send("rx%d" % t, T["x%d" % t][:], T.x0[:], d, tab_engines(core, d), "x0", 14.0, "x%d" % t, after=tab_ready + after,
+             n_in=len(tab_engines(dst(t), core)))
+
+    send_table(1, [])
+    for nm, i in (("sl", 1), ("pl", 0), ("ll", 2)):
+        v(cp(T.u16l[:, 256 * i:256 * i + 256], T["i_" + nm][:]), 256, r=["i_" + nm], w=["u16l%d0" % i, "u16l%d1" % i])
+    v(cp(T.u16q[:, 0:256], T.i_ql[:]), 256, r=["i_ql"], w=["u16q00", "u16q01"])
+    for nm in ("ll", "ql", "pl", "sl"):
+        v(cp(T["f_" + nm][:], T["i_" + nm][:]), 256, r=["i_" + nm], w=["f_" + nm])
+
+    def first_page_form(h):
+        hs = slice(128 * h, 128 * h + 128)
+        mm([MM(T.bE[:, 0:128], T.f_ll[:, hs], T.i32[:], True, True)], 512, r=["f_ll", "i32"], w=["bE0"], b=["bE"])
+        mm([MM(T.bE[:, 128:256], T.f_ql[:, hs], T.i32[:], True, True)], 512, r=["f_ql", "i32"], w=["bE1"], b=["bE"])
+        mm([MM(T.bE[:, 256:384], T.f_pl[:, hs], T.i32[:], True, True)], 512, r=["f_pl", "i32"], w=["bE2"], b=["bE"])
+        mm([MM(T.bE[:, 384:512], T.f_sl[:, hs], T.i32[:], True, True)], 512, r=["f_sl", "i32"], w=["bE3"], b=["bE"])
+        v(ts(cb("lh", 0, h), T.bE[:, 0:128], 2048.0, OP.subtract), 128, r=["bE0"], w=["lh0%d" % h], b=["bE"])
+        v(ts(cb("qh", 0, h), T.bE[:, 128:256], 2048.0, OP.subtract), 128, r=["bE1"], w=["qh0%d" % h], b=["bE"])
+        s(act(cb("qst", 0, h), T.bE[:, 128:256], AF.Copy, 4096.0), 128, r=["bE1"], w=["qst0%d" % h], b=["bE"])
+        for i, c in ((2, 0), (0, 2), (1, 3)):
+            s(act(cb("lst", i, h), T.bE[:, 128 * c:128 * c + 128], AF.Copy, 8192.0), 128, r=["bE%d" % c], w=["lst%d%d" % (i, h)], b=["bE"])
+
+    P = 2048 // PCS
+    first, dn = {}, [0]
+
+    def tabs(t):
+        x = "x%d" % t
+        e = ["xe0"] if t == 0 else [x]
+        late = [first[(t - 1, 1)]] if t else []
+        v(ts(T["thm%d" % t][:, 0:128], T.ib[:], T[x][:, 4096:4097], OP.mult), 128, 0.5, r=["ib"] + e, w=["thm%d" % t], after=late)
+        v(ms(T["thm%d" % t][:, 128:512], 0.0), 384, 0.5, w=["thz%d" % t])
+        v(ts(T["thm%d" % t][:, 512:640], T.ib[:], T[x][:, 4097:4098], OP.mult), 128, 0.5, r=["ib"] + e, w=["thn%d" % t], after=late)
+        v(ts(T["wb%d" % t][:], T.b128[:], T[x][:, 4098:4099], OP.mult), 128, 0.5, r=["b128"] + e, w=["wb%d" % t], after=late)
+
+    def big(t, h):
+        hh = str(h)
+        x = "x%d" % (t % 4)
+        win = T[x][:, 0:4096]
+        B = {n: T[n + hh] for n in ("sg", "lg", "da", "dd", "ra", "rd", "ab", "ac", "ao", "mx")}
+
+        def off(buf, i, j):
+            c = i * 256 + h * 128 + j * (128 // PCS)
+            return T[buf][:, c:c + 128 // PCS]
+
+        K = lambda n, j: n + hh + "p%d" % j
+        for j in range(PCS):
+            sl = slice(P * j, P * j + P)
+            s(act(B["sg"][:, sl], win.indirect(off("u16l", t + 1, j)), AF.Copy), P * GATH, r=[x, "u16l%d%d" % (t + 1, h)], w=[K("sg", j)])
+        for j in range(PCS):
+            sl = slice(P * j, P * j + P)
+            s(act(B["lg"][:, sl], win.indirect(off("u16l", t + 2, j)), AF.Copy), P * GATH, r=[x, "u16l%d%d" % (t + 2, h)], w=[K("lg", j)])
+        for j in range(PCS):
+            sl = slice(P * j, P * j + P)
+            o = v(tt(B["da"][:, sl], win.indirect(off("u16l", t, j)), B["sg"][:, sl], OP.subtract), P * GATH,
+                  r=[x, "u16l%d%d" % (t, h), K("sg", j)], w=[K("da", j)])
+            first[(t, h)] = o
+            v(ts(B["ra"][:, sl], B["da"][:, sl], 0.0, OP.max), P, 0.5, r=[K("da", j)], w=[K("ra", j)])
+        for j in range(PCS):
+            sl = slice(P * j, P * j + P)
+            v(lambda a=B["mx"][:, sl], b=B["lg"][:, sl]: g.vector.tensor_tensor_scan(a, T.msk[:], b, 0.0, OP.mult, OP.max), P, 0.5,
+              r=["msk", K("lg", j)], w=[K("mx", j)])
+        mo = "mo%d%d" % (t, h)
+        s(act(cb("mo", t, h), B["mx"][:, 15::16], AF.Copy), 128, r=[K("mx", j) for j in range(PCS)], w=[mo])
+        d2 = dst(2)
+        send("rm%d%d" % (t, h), cb("mi", t, h), cb("mo", t, h), d2, topo.engines(core, d2)[4:8], mo, 4.0, "mi%d%d" % (t, h))
+        for j in range(PCS):
+            sl = slice(P * j, P * j + P)
+            v(tt(B["dd"][:, sl], win.indirect(off("u16q", t, j)), B["sg"][:, sl], OP.subtract), P * GATH,
+              r=[x, "u16q%d%d" % (t, h), K("sg", j)], w=[K("dd", j)])
+            v(ts(B["rd"][:, sl], B["dd"][:, sl], 0.0, OP.max), P, 0.5, r=[K("dd", j)], w=[K("rd", j)])
+        def size_b(j):
+            d, sl, gp = "d%d" % (dn[0] % 3), slice(512 * j, 512 * j + 512), 512 * j // P
+            for nm, mat, st, sp in (("sg", "ib", True, False), ("lg", "nib", False, True)):
+                mm([MM(T[d][:], T[mat][:], B[nm][:, sl], st, sp)], 512, r=[K(nm, gp), mat] + ([] if st else [d]), w=[d], b=[d])
+            s(act(B["ab"][:, sl], T[d][:], AF.Abs), 512, r=[d], w=["ab%sp%d" % (hh, j)], b=[d])
+            dn[0] += 1
+
+        def size_c(j):
+            d, sl, gp = "d%d" % (dn[0] % 3), slice(512 * j, 512 * j + 512), 512 * j // P
+            for nm, mat in (("sg", "ib"), ("da", "ib"), ("lg", "nib")):
+                mm([MM(T[d][:], T[mat][:], B[nm][:, sl], nm == "sg", nm == "lg")], 512, r=[K(nm, gp), mat] + ([] if nm == "sg" else [d]), w=[d], b=[d])
+            s(act(B["ac"][:, sl], T[d][:], AF.Abs), 512, r=[d], w=["ac%sp%d" % (hh, j)], b=[d])
+            dn[0] += 1
+
+        for j in range(4):
+            size_b(j)
+        for j in range(4):
+            size_c(j)
+        e = "e%d%d" % (t, h)
+        for j in range(4):
+            d = "d%d" % ((dn[0] + j) % 3)
+            fn = []
+            for i in range(4):
+                o_ = T[d][:, 128 * i:128 * i + 128]
+                fn += [MM(o_, T.ib[:], B["lg"][:, 4 * j + i::16], True, False), MM(o_, T.nib[:], T[e][:, 0:128], False, True)]
+            mm(fn, 1024, r=[K("lg", jj) for jj in range(PCS)] + [e, "ib", "nib"], w=[d], b=[d])
+            s(act(B["ao"][:, 512 * j:512 * j + 512], T[d][:], AF.Abs), 512, r=[d], w=["ao%sp%d" % (hh, j)], b=[d])
+        dn[0] += 4
+
+    def logic(t, h):
+        hh, n = str(h), 128
+        tm = t % 4
+        B = {nm: T[nm + hh] for nm in ("da", "dd", "ra", "rd", "ab", "ac", "ao")}
+        A, Bb, D, E = T["bA" + hh], T.bB, T.bD, T.bE
+        half[0] = hh
+        k_ = lambda nm: nm + hh
+        pcs = lambda nm: [nm + hh + "p%d" % j for j in range(4 if nm[0] == "a" else PCS)]
+        fl = T["fl" + hh]
+        it = lambda nm: cb("itmp", ITMP.index(nm), h)
+        ft = lambda nm: cb("ftmp", FTMP.index(nm), h)
+        e, eo, mi = "e%d%d" % (t, h), "eo%d%d" % (t, h), "mi%d%d" % (t, h)
+        if t == 0:
+            first_page_form(h)
+        mm([MM(A[:], one_row, T.rowlo[0:1, :], True, False)], 512, r=["one"] + CK, w=["A"], b=["bA"])
+        mm([MM(A[:, 384:512], T.one[:], T["thm%d" % tm][:, 0:128], False, False)], 128, r=["one", "thm%d" % tm], a=["A"], b=["bA"])
+
+        def sums(nm, a, b):
+            fn = []
+            for k in range(16):
+                lt = B[nm][:, 128 * k:128 * k + 128] if nm == "ao" else B[nm][:, k::16]
+                fn.append(MM(A[:, a + k:b:16], lt, T.fun[:, FUN[nm][0]:FUN[nm][1]], False, False))
+            mm(fn, 64 * len(fn), r=pcs(nm) + FK, a=["A"], b=["bA"])
+
+        sums("ra", 256, 384)
+        sums("da", 256, 384)
+        sums("rd", 0, 128)
+        sums("dd", 0, 128)
+        sums("ab", 0, 384)
+        sums("ac", 128, 384)
+        sums("ao", 384, 512)
+        mm([MM(A[:], T.one[:], T["thm%d" % tm][:, 128:640], False, True)], 512, r=["one", "thn%d" % tm, "thz%d" % tm], w=["A"], b=["bA"])
+        X2, X1, XF, X3 = [A[:, 128 * i:128 * i + 128] for i in range(4)]
+        mm([MM(D[:, 0:128], T[e][:, 0:128], T["wb%d" % tm][:], True, True)], 128, r=[e, "wb%d" % tm], w=["Du"], b=["bD"])
+        if h == 0:
+            if t == 0:
+                v(cp(T.ka[:], T.k37[:]), n, r=["k37"], w=["ka"])
+            else:
+                v(ts(T.ka[:], T.k37[:], T["e%d1" % t][:, 128:129], OP.add), n, r=["k37", "e%d1" % t], w=["ka"])
+        lh, qo = cb("lh", t, h), cb("qst", t, h)
+        PL, PY, PLm, PLQ = [Bb[:, 128 * i:128 * i + 128] for i in range(4)]
+        mm([MM(PL, one_row, T.rowb[0:1, 0:128], True, False), MM(PL, T.i16[:], lh, False, True),
+            MM(PY, one_row, T.rowb[0:1, 0:128], True, False), MM(PY, T.i16[:], lh, False, False), MM(PY, T.i16[:], T.ka[:], False, True),
+            MM(PLm, one_row, T.rowb[0:1, 128:256], True, False), MM(PLm, T.i16[:], lh, False, True),
+            MM(PLQ, T.i16[:], lh, True, False), MM(PLQ, T.n16[:], cb("qh", t, h), False, True)], 9 * 128,
+           r=["one", "i16", "n16", "lh%d%d" % (t, h), "qh%d%d" % (t, h), "ka"] + CB_, w=["B"], b=["bB"])
+        v(cp(it("ui"), D[:, 0:128]), n, r=["Du"], w=[k_("ui")], b=["bD"])
+        v(ts(it("uj"), it("ui"), 4095, OP.bitwise_and), n, r=[k_("ui")], w=[k_("uj")])
+        v(tt(it("z"), it("uj"), PL, OP.mult), n, r=[k_("uj"), "B"], w=[k_("z")], b=["bB"])
+        v(ts(it("zs"), it("z"), 5, OP.arith_shift_right), n, r=[k_("z")], w=[k_("zs")])
+        v(tt(it("y"), it("zs"), PY, OP.add), n, r=[k_("zs"), "B"], w=[k_("y")], b=["bB"])
+        v(ts(it("ch"), it("y"), 4095, OP.bitwise_and), n, r=[k_("y")], w=[k_("ch")])
+        ms_, fz = T.msk[:, 0:128], T["fz" + hh]
+        v(lambda: g.vector.tensor_tensor_scan(ft("sc"), ms_, XF, 0.0, OP.mult, OP.add), n, r=["A", "msk"], w=[k_("sc")], b=["bA"])
+        v(ts(fz[:, 0::16], T.ftmp[:, FTMP.index("sc") * 256 + 128 * h + 15:FTMP.index("sc") * 256 + 128 * h + 128:16], 0.0, OP.is_lt), 8,
+          r=[k_("sc"), "fz0" + hh], w=[k_("fz")])
+        v(lambda: g.vector.tensor_tensor_scan(fl[:], ms_, fz[:], 0.0, OP.mult, OP.add), n, 0.5, r=["msk", k_("fz")], w=[k_("fl") + "a"])
+        v(ts(T["gf" + hh][:], fl[:], 65536.0, OP.mult, 65536.0, OP.subtract), n, 0.5, r=[k_("fl") + "a"], w=[k_("gf")])
+        FL = [k_("fl") + "a"]
+        mm([MM(D[:, 256:384], T.ib[:], T[e][:, 0:128], True, False), MM(D[:, 256:384], T.nib[:], cb("mi", t, h), False, True),
+            MM(D[:, 384:512], T.hib[:], T[e][:, 0:128], True, False), MM(D[:, 384:512], T.hib[:], cb("mi", t, h), False, False),
+            MM(D[:, 384:512], one_row, T.rowq[0:1, :], False, False), MM(D[:, 384:512], fl[:], T.im512[:], False, True),
+            MM(D[:, 128:256], fl[:], T.i1024[:], True, True)], 7 * 128,
+           r=FL + [e, mi, "ib", "nib", "hib", "one", "rowq0", "im512", "i1024"], w=["De"], b=["bD"])
+        s(act(ft("absd"), D[:, 256:384], AF.Abs), n, r=["De"], w=[k_("absd")], b=["bD"])
+        v(ts(ft("t2"), D[:, 384:512], MAGIC, OP.add, MAGIC, OP.subtract), n, r=["De"], w=[k_("t2")], b=["bD"])
+        v(tt(E[:, 0:128], ft("absd"), D[:, 128:256], OP.min), n, r=["De", k_("absd")], w=["bE0"], b=["bD", "bE"])
+        v(tt(T[eo][:, 0:128], ft("t2"), E[:, 0:128], OP.max), n, r=[k_("t2"), "bE0"], w=[eo], b=["bE"])
+        if t < V - 1:
+            if h == 1:
+                mm([MM(D[:, 0:1], T.one[:], T["fl%d" % a][:, 16 * q:16 * q + 1], (a, q) == (0, 0), (a, q) == (1, 7)) for a in range(2) for q in range(8)],
+                   1024, r=FL + ["fl0a", "one"], w=["Du"], b=["bD"])
+                v(cp(T.acol[:, 0:1], D[:, 0:1]), 1, r=["Du"], w=["ac0"], b=["bD"])
+                v(ts(T.acol[:, 1:2], T.acol[:, 0:1], 31, OP.bitwise_and), 1, r=["ac0"], w=["ac1"])
+                v(ms(T[eo][:, 128:144], 0.0), 16, w=[eo + "A"])
+                v(cp(T[eo][:, 128:129], T.acol[:, 1:2]), 1, r=["ac1"], w=[eo + "A"])
+            else:
+                v(ms(T[eo][:, 128:144], 0.0), 16, w=[eo + "A"])
+            d1 = dst(-1)
+            en = "e%d%d" % (t + 1, h)
+            send("re%d%d" % (t + 1, h), T[en][:], T[eo][:], d1, topo.engines(core, d1)[4:8], eo, 4.0, en, after=[last_w[eo + "A"]])
+        else:
+            op("Y", 0.1, [lambda: g.sync.dma_start(T.ye[:, 128 * h:128 * h + 128], T[eo][:, 0:128])], r=[eo], sig=("d_ye%d" % h, 16), lat=2.0)
+        pst = cb("lst", t, h)
+        v(tt(ft("m3"), it("ch"), X3, OP.min), n, r=[k_("ch"), "A"], w=[k_("m3")], b=["bA"])
+        v(tt(ft("r3"), ft("m3"), PLm, OP.max), n, r=[k_("m3"), "B"], w=[k_("r3")], b=["bB"])
+        v(tt(E[:, 0:128], qo, X2, OP.min), n, r=["qst%d%d" % (t, h), "A"], w=["bE0"], b=["bA", "bE"])
+        v(tt(E[:, 128:256], pst, X1, OP.min), n, r=["lst%d%d" % (t, h), "A"], w=["bE1"], b=["bA", "bE"])
+        v(tt(ft("m1"), T["gf" + hh][:], E[:, 128:256], OP.add), n, r=[k_("gf"), "bE1"], w=[k_("m1")], b=["bE"])
+        v(tt(E[:, 0:128], ft("r3"), E[:, 0:128], OP.max), n, r=[k_("r3"), "bE0"], w=["bE0"], b=["bE"])
+        v(tt(it("r1"), ft("m1"), E[:, 0:128], OP.max), n, r=[k_("m1"), "bE0"], w=[k_("r1")], b=["bE"])
+        nw = it("nw")
+        v(ts(nw, it("r1"), 4095, OP.bitwise_and), n, r=[k_("r1")], w=[k_("nw")])
+        v(ts(cb("lh", t + 1, h), nw, 2048.0, OP.subtract), n, r=[k_("nw")], w=["lh%d%d" % (t + 1, h)])
+        if t + 3 < 5:
+            v(ts(cb("lst", t + 3, h), nw, 8192.0, OP.add), n, r=[k_("nw")], w=["lst%d%d" % (t + 3, h)])
+        qn = cb("qst", t + 1, h)
+        v(tt(ft("ne"), nw, PL, OP.not_equal), n, r=[k_("nw"), "B"], w=[k_("ne")], b=["bB"])
+        v(tt(E[:, 128:256], ft("ne"), PLQ, OP.mult), n, r=[k_("ne"), "B"], w=["bE1"], b=["bB", "bE"])
+        v(tt(qn, qo, E[:, 128:256], OP.add), n, r=["qst%d%d" % (t, h), "bE1"], w=["qst%d%d" % (t + 1, h)], b=["bE"])
+        mm([MM(E[:, 256:384], cb("lh", t + 1, h), T.i16[:], True, True)], 128, r=["i16", "lh%d%d" % (t + 1, h)], w=["bE2"], b=["bE"])
+        if t < V - 1:
+            v(ts(cb("u16l", t + 3, h), E[:, 256:384], 2048.0, OP.add), n, r=["bE2"], w=["u16l%d%d" % (t + 3, h)], b=["bE"])
+        v(ts(cb("qh", t + 1, h), qn, 6144.0, OP.subtract), n, r=["qst%d%d" % (t + 1, h)], w=["qh%d%d" % (t + 1, h)])
+        mm([MM(E[:, 384:512], cb("qh", t + 1, h), T.i16[:], True, True)], 128, r=["i16", "qh%d%d" % (t + 1, h)], w=["bE3"], b=["bE"])
+        if t < V - 1:
+            v(ts(cb("u16q", t + 1, h), E[:, 384:512], 2048.0, OP.add), n, r=["bE3"], w=["u16q%d%d" % (t + 1, h)], b=["bE"])
+        if t >= 2:
+            o_ = cb("outs", t - 2, h)
+            nm = ("yp", "ys", "yl")[t - 2]
+            s(act(o_, E[:, 256:384], AF.Copy, 2048.0), n, r=["bE2"], w=["outs%d%d" % (t - 2, h)], b=["bE"])
+            op("Y", 0.1, [lambda: g.sync.dma_start(T[nm][:, 128 * h:128 * h + 128], o_)], r=["outs%d%d" % (t - 2, h)], sig=("d_%s%d" % (nm, h), 16), lat=2.0)
+        if t == V - 1:
+            oq = cb("outs", 3, h)
+            s(act(oq, E[:, 384:512], AF.Copy, 2048.0), n, r=["bE3"], w=["outs3%d" % h], b=["bE"])
+            op("Y", 0.1, [lambda: g.sync.dma_start(T.yq[:, 128 * h:128 * h + 128], oq)], r=["outs3%d" % h], sig=("d_yq%d" % h, 16), lat=2.0)
+
+    for t in range(V):
+        if t < 4:
+            tabs(t)
+        for h in range(H2):
+            big(t, h)
+            logic(t, h)
+        if t == 0:
+            send_table(2, [])
+            send_table(3, [first[(0, 1)]])
+    return ops
+
+
+def _order(ops):
+    n = len(ops)
+    succ = [[] for _ in range(n)]
+    for o in ops:
+        for d in o["d"]:
+            succ[d].append(o["i"])
+    prio = [0.0] * n
+    for o in reversed(ops):
+        m = 0.0
+        for k in succ[o["i"]]:
+            if prio[k] > m:
+                m = prio[k]
+        prio[o["i"]] = m + o["c"] + o["lat"] + 0.05
+    left = [len(o["d"]) for o in ops]
+    ready_t = [0.0] * n
+    free, ready, order = {}, {}, {}
+    for o in ops:
+        if not left[o["i"]]:
+            ready.setdefault(o["q"], []).append(o["i"])
+    done = 0
+    while done < n:
+        best = None
+        for q, lst in ready.items():
+            f = free.get(q, 0.0)
+            for i in lst:
+                st = max(f, ready_t[i])
+                key = (st, -prio[i])
+                if best is None or key < best[0]:
+                    best = (key, q, i)
+        (st, _), q, i = best
+        o = ops[i]
+        ready[q].remove(i)
+        order.setdefault(q, []).append(o)
+        fin = st + o["c"]
+        if q != "R":
+            free[q] = fin
+        for k in succ[i]:
+            ready_t[k] = max(ready_t[k], fin + o["lat"] + 0.08)
+            left[k] -= 1
+            if not left[k]:
+                ready.setdefault(ops[k]["q"], []).append(k)
+        o["st"] = st
+        done += 1
+    return order
+
+
+def rank_program(g, core, T, topo):
+    if T.rank_of(core) is None:
+        return
+    ops = _plan(g, core, T, topo)
+    order = _order(ops)
+    qs = {"T": g.tensor, "V": g.vector, "S": g.scalar, "G": g, "Y": g.sync}
+    qsem = {"T": "sT", "V": "sV", "S": "sS", "G": "sG"}
+    count = {q: 0 for q in qs}
+    known = {q: {} for q in qs}
+    sent = 0
+    glob = [o for q in order for o in order[q]]
+    for q in ("T", "V", "S", "G"):
+        c = 0
+        for o in order[q]:
+            if o["sig"] is None:
+                c += len(o["f"])
+                o["val"] = (qsem[q], c)
+            elif o["sig"][0] == "send":
+                o["val"] = None
+    for q in ("Y", "R"):
+        for o in order[q]:
+            o["val"] = o["sig"]
+    for o in sorted(glob, key=lambda o: (o["st"], o["i"])):
+        o["w"] = []
+        if o["q"] == "R":
+            o["clk"] = {o["val"][0]: o["val"][1]}
+            continue
+        kn = known[o["q"]]
+        need = {}
+        for d in o["d"]:
+            x = ops[d]
+            if x["val"] is None or (x["q"] == "T" and o["q"] == "T"):
+                continue
+            sm, vl = x["val"]
+            if kn.get(sm, 0) < vl and need.get(sm, (0, None))[0] < vl:
+                need[sm] = (vl, x)
+        for sm in sorted(need, key=lambda m: -need[m][1]["st"]):
+            vl, x = need[sm]
+            if kn.get(sm, 0) < vl:
+                o["w"].append((sm, vl))
+                for a, b in list(x["clk"].items()) + [(sm, vl)]:
+                    if kn.get(a, 0) < b:
+                        kn[a] = b
+        o["clk"] = dict(kn)
+        if o["val"] is not None:
+            o["clk"][o["val"][0]] = o["val"][1]
+    for q in qs:
+        eng = qs[q]
+        for o in order.get(q, []):
+            for sm, vl in o["w"]:
+                eng.wait_ge(T.sem[sm], vl)
+            for f in o["f"]:
+                ins = f()
+                if o["sig"] is None:
+                    ins.then_inc(T.sem[qsem[q]], 1)
+                elif o["sig"][0] == "send":
+                    sent += o["sig"][1]
+                else:
+                    ins.then_inc(T.sem[o["sig"][0]], 16)
+    for q in ("T", "V", "S", "G"):
+        tot = max([o["val"][1] for o in order[q] if o["val"] is not None] + [0])
+        g.sync.wait_ge(T.sem[qsem[q]], tot)
+    for nm in STORES:
+        g.sync.wait_ge(T.sem["d_" + nm], 16)
+    g.wait_ge(T.sem["lsem"], sent)

@@ -1,10 +1,15 @@
 import numpy as np
-from concourse.mybir import AluOpType as OP, ActivationFunctionType as AF
+from concourse.mybir import AluOpType as OP, ActivationFunctionType as AF, AxisListType as AX
 
 V, H2 = 5, 2
 PCS = 2
 PE_NS, CY_NS, GATH = 0.4167, 0.83, 1.5
-MAGIC = 8388608.0
+LAT, WAKE = 5.0, 0.08
+SPREAD, SEED, TRIES, TURNS = 2.0, 849, 6, 6
+SC = 2.0 ** 23
+CF, CQ, CP = 8192.0, 2.0 ** 20, 2.0 ** 21
+GATE = 2.0 ** 22
+OMAX = set()
 
 SCRATCH, SEMAPHORES = {}, ["sT", "sV", "sS", "sG", "lsem"]
 
@@ -17,14 +22,14 @@ for _n in ("d0", "d1", "d2", "bA0", "bA1", "bB", "bD", "bE"):
     _buf(_n, 512, "float32", "psum")
 for _t in range(4):
     _buf("x%d" % _t, 4096 + 16, "bfloat16")
-    _buf("thm%d" % _t, 640, "bfloat16")
+    _buf("thm%d" % _t, 256, "bfloat16")
     _buf("wb%d" % _t, 128, "bfloat16")
 for _h in range(2):
     for _n in ("sg", "lg", "da", "dd", "ra", "rd", "ab", "ac", "ao", "mx"):
         _buf(_n + str(_h), 2048, "bfloat16")
-    for _n in ("fl", "fz", "gf"):
+    for _n in ("fl", "fz", "absd"):
         _buf(_n + str(_h), 128, "bfloat16")
-ITMP, FTMP = ("ui", "uj", "z", "zs", "y", "ch", "r1", "nw"), ("m3", "r3", "m1", "ne", "absd", "t2", "sc")
+ITMP, FTMP = ("ui", "uj", "z", "zs", "y", "r1", "nw", "t2"), ("m3", "r3", "m1", "ne", "sc")
 _buf("itmp", len(ITMP) * 256, "int32")
 _buf("ftmp", len(FTMP) * 256, "float32")
 _buf("mo", V * 256, "bfloat16")
@@ -47,24 +52,25 @@ for _t in range(V + 1):
 SEMAPHORES += ["rx1", "rx2", "rx3"]
 for _n in ("pl", "sl", "ll", "ql"):
     _buf("i_" + _n, 256, "int32")
-    _buf("f_" + _n, 256, "float32")
+    _buf("f_" + _n, 256, "float16")
 _buf("i_tw", 2, "int32")
 _buf("i_th", 2, "int32")
 _buf("ka", 128, "float16")
 _buf("k37", 128, "float32")
 _buf("acol", 2, "int32")
+_buf("cnt", 1, "float32")
+_buf("onec", 128, "bfloat16")
 _buf("one32", 128, "float32")
 _buf("i32", 128, "float32")
 _buf("i16", 128, "float16")
 _buf("n16", 128, "float16")
-for _n in ("one", "ib", "nib", "hib", "i1024", "im512", "bt", "b128"):
+for _n in ("one", "ib", "nib", "i1024", "im512", "bt", "b128"):
     _buf(_n, 128, "bfloat16")
 _buf("msk", 2048 // PCS, "bfloat16")
 _buf("mskk", 2048 // PCS, "bfloat16")
-_buf("fun", 80, "bfloat16")
+_buf("fun", 96, "bfloat16")
 _buf("rowb", 256, "bfloat16")
 _buf("rowlo", 512, "bfloat16")
-_buf("rowq", 128, "bfloat16")
 LOADS = ["sl", "xt", "pl", "th", "wt", "ll", "ql", "ed0", "ed1"]
 STORES = ["%s%d" % (_n, _h) for _n in ("yp", "ys", "yl", "yq", "ye") for _h in range(2)]
 SEMAPHORES += ["d_" + _n for _n in LOADS + STORES]
@@ -145,12 +151,12 @@ def _plan(g, core, T, topo):
     def load(name, out, in_, key):
         return op("Y", 0.1, [lambda: g.sync.dma_start(out, in_)], w=[key], sig=("d_" + name, 16), lat=4.0 if name == "xt" else 2.2)
 
-    def send(name, out, in_, dst, eng, key, lat, rkey, after=(), n_in=None):
+    def send(name, out, in_, dst, eng, key, lat, rkey, after=()):
         eng = [e for e in eng]
         m = sum(1 << e for e in eng)
         rid, pid, _ = topo.addr(dst)
         so = op("G", 1.3, [lambda: g.remote_dma(out, in_, T.sem[name], T.sem["lsem"], pid, rid, m)], r=[key], sig=("send", len(eng)), after=after)
-        op("R", 0.0, [], w=[rkey], sig=(name, n_in or len(eng)), after=[so], lat=lat)
+        op("R", 0.0, [], w=[rkey], sig=(name, len(eng)), after=[so], lat=lat)
         return so
 
     def dst(k):
@@ -171,31 +177,31 @@ def _plan(g, core, T, topo):
     load("ed1", T.e01[:, 0:128], T.ed[:, 128:256], "e01")
     ms = lambda ap, c: (lambda: g.vector.memset(ap, c))
     v(ms(T.one32[:], 1.0), 128, w=["one32"])
-    v(ms(T.one[:], 1.0), 128, w=["one"])
+    v(ms(T.one[:], 1.0), 128, 0.5, w=["one"])
+    v(ms(T.onec[:], 1.0 / GATE), 128, 0.5, w=["onec"])
     gq = lambda fn, n, **kw: op("G", 0.2 + n * 2 * CY_NS / 1000, [fn], **kw)
     gq(lambda: g.affine_select(T.i32[:], T.one32[:], [[-1, 128]], OP.is_equal, 0.0, 0, 1), 128, r=["one32"], w=["i32"])
     gq(lambda: g.affine_select(T.bt[:], T.one[:], [[-16, 8], [0, 16]], OP.is_ge, 0.0, 0, 1), 128, r=["one"], w=["bt"])
     gq(lambda: g.affine_select(T.b128[:], T.bt[:], [[16, 8], [0, 16]], OP.is_ge, 0.0, 15, -1), 128, r=["bt"], w=["b128"])
     gq(lambda: g.iota(T.mskk[:], [[0, 128 // PCS], [1, 16]], 0, 0, allow_small_or_imprecise_dtypes=True), 2048 // PCS, w=["mskk"])
     gq(lambda: g.iota(T.k37[:], [[0, 8], [37, 16]], 0, 0, allow_small_or_imprecise_dtypes=True), 128, w=["k37"])
-    for nm, c in (("ib", 1.0), ("nib", -1.0), ("hib", 0.5), ("i1024", 1024.0), ("im512", -512.0), ("i16", 1.0), ("n16", -1.0)):
+    for nm, c in (("ib", 1.0), ("nib", -1.0), ("i1024", 1024.0 / GATE), ("im512", -512.0 / GATE), ("i16", 1.0), ("n16", -1.0)):
         if nm in ("i16", "n16"):
             v(ts(T[nm][:], T.i32[:], c, OP.mult), 128, r=["i32"], w=[nm])
         else:
             s(act(T[nm][:], T.i32[:], AF.Copy, 0.0, c), 128, r=["i32"], w=[nm])
     v(ts(T.msk[:], T.mskk[:], 0.0, OP.is_gt), 2048 // PCS, 0.5, r=["mskk"], w=["msk"])
-    SC = 32768.0
     FUN = {"ab": (0, 24), "ac": (24, 40), "ra": (40, 48), "da": (48, 56), "rd": (56, 64), "dd": (64, 72), "ao": (72, 80)}
-    for i, c in enumerate((SC, SC, -2.0, -SC, 2.0, -2.0, 1.0, -2 * SC, SC, SC)):
+    for i, c in enumerate((SC, SC, -2.0, -SC, 2.0, -2.0, 1.0, -2 * SC, SC, SC, 2 * SC, -SC)):
         s(act(T.fun[:, 8 * i:8 * i + 8], T.b128[:, 0::16], AF.Copy, 0.0, c), 8, r=["b128"], w=["fun%d" % i])
     for nm, a, b, c in (("rowlo", 0, 256, -SC / 2), ("rowlo", 256, 384, 0.0), ("rowlo", 384, 512, SC / 2),
-                        ("rowb", 0, 128, 2048.0), ("rowb", 128, 256, -2048.0), ("rowq", 0, 128, -0.25)):
+                        ("rowb", 0, 128, 2048.0), ("rowb", 128, 256, 2048.0 + CF)):
         v(ms(T[nm][0:1, a:b], c), b - a, w=[nm + str(a)])
     for h in range(H2):
         v(ms(T["fz%d" % h][:], 0.0), 128, 0.5, w=["fz0%d" % h])
     CK = ["rowlo0", "rowlo256", "rowlo384"]
     CB_ = ["rowb0", "rowb128"]
-    FK = ["fun%d" % i for i in range(10)]
+    FK = ["fun%d" % i for i in range(12)]
     one_row = T.one[0:1, :]
     v(ts(T.i_th[:, 0:1], T.i_tw[:, 0:1], 4, OP.arith_shift_right), 1, r=["i_th"], w=["thh"])
     v(ts(T.i_th[:, 1:2], T.i_tw[:, 0:1], 15, OP.bitwise_and), 1, r=["i_th"], w=["thl"])
@@ -205,44 +211,56 @@ def _plan(g, core, T, topo):
     v(cp(T.x0[:, 4098:4099], T.i_tw[:, 1:2]), 1, r=["i_wt"], w=["xe0"])
     tab_ready = [o for o in ops if o["i"] in (last_w["x0"]["i"], last_w["xe0"]["i"])]
 
+    first = {}
+
+    def relayed(home, t):
+        c, c1, c0 = T.cores[home], T.cores[(home + 1) % N], T.cores[(home + t) % N]
+        return t > 1 and topo.chip(c) != topo.chip(c0) and topo.chip(c) == topo.chip(c1)
+
     def send_table(t, after):
         def tab_engines(a, b):
             en = topo.engines(a, b)
-            return en[8:16] if len(en) >= 16 else (en[0:8] if t == 1 else en[0:4])
+            return en if len(en) >= 16 or t == 1 else en[0:8:2]
 
-        d = dst(-t)
-        send("rx%d" % t, T["x%d" % t][:], T.x0[:], d, tab_engines(core, d), "x0", 14.0, "x%d" % t, after=tab_ready + after,
-             n_in=len(tab_engines(dst(t), core)))
+        back = (rank - t) % N
+        outs = [] if relayed(back, t) else [(T.cores[back], "x0", tab_ready)]
+        if relayed((rank - 1) % N, t):
+            outs.append((dst(-1), "x%d" % (t - 1), []))
+        for d, src, rd in outs:
+            en = tab_engines(core, d)
+            m = sum(1 << k for k in en)
+            rid, pid, _ = topo.addr(d)
+            op("G", 1.3, [lambda src=src, rid=rid, pid=pid, m=m: g.remote_dma(T["x%d" % t][:], T[src][:], T.sem["rx%d" % t], T.sem["lsem"], pid, rid, m)],
+               r=[src], sig=("send", len(en)), after=rd + (after if src == "x0" else [first[(t - 2, 1)]]))
+        frm = dst(1) if relayed(rank, t) else dst(t)
+        op("R", 0.0, [], w=["x%d" % t], sig=("rx%d" % t, len(tab_engines(frm, core))), after=tab_ready + after, lat=16.0 if t == 1 else 30.0)
 
     send_table(1, [])
     for nm, i in (("sl", 1), ("pl", 0), ("ll", 2)):
         v(cp(T.u16l[:, 256 * i:256 * i + 256], T["i_" + nm][:]), 256, r=["i_" + nm], w=["u16l%d0" % i, "u16l%d1" % i])
     v(cp(T.u16q[:, 0:256], T.i_ql[:]), 256, r=["i_ql"], w=["u16q00", "u16q01"])
     for nm in ("ll", "ql", "pl", "sl"):
-        v(cp(T["f_" + nm][:], T["i_" + nm][:]), 256, r=["i_" + nm], w=["f_" + nm])
+        v(ts(T["f_" + nm][:], T["i_" + nm][:], 2048.0, OP.subtract), 256, r=["i_" + nm], w=["f_" + nm])
 
     def first_page_form(h):
         hs = slice(128 * h, 128 * h + 128)
-        mm([MM(T.bE[:, 0:128], T.f_ll[:, hs], T.i32[:], True, True)], 512, r=["f_ll", "i32"], w=["bE0"], b=["bE"])
-        mm([MM(T.bE[:, 128:256], T.f_ql[:, hs], T.i32[:], True, True)], 512, r=["f_ql", "i32"], w=["bE1"], b=["bE"])
-        mm([MM(T.bE[:, 256:384], T.f_pl[:, hs], T.i32[:], True, True)], 512, r=["f_pl", "i32"], w=["bE2"], b=["bE"])
-        mm([MM(T.bE[:, 384:512], T.f_sl[:, hs], T.i32[:], True, True)], 512, r=["f_sl", "i32"], w=["bE3"], b=["bE"])
-        v(ts(cb("lh", 0, h), T.bE[:, 0:128], 2048.0, OP.subtract), 128, r=["bE0"], w=["lh0%d" % h], b=["bE"])
-        v(ts(cb("qh", 0, h), T.bE[:, 128:256], 2048.0, OP.subtract), 128, r=["bE1"], w=["qh0%d" % h], b=["bE"])
-        s(act(cb("qst", 0, h), T.bE[:, 128:256], AF.Copy, 4096.0), 128, r=["bE1"], w=["qst0%d" % h], b=["bE"])
+        for c, nm in enumerate(("ll", "ql", "pl", "sl")):
+            mm([MM(T.bE[:, 128 * c:128 * c + 128], T["f_" + nm][:, hs], T.i16[:], True, True)], 128, r=["f_" + nm, "i16"], w=["bE%d" % c], b=["bE"])
+        v(cp(cb("lh", 0, h), T.bE[:, 0:128]), 128, r=["bE0"], w=["lh0%d" % h], b=["bE"])
+        v(cp(cb("qh", 0, h), T.bE[:, 128:256]), 128, r=["bE1"], w=["qh0%d" % h], b=["bE"])
+        s(act(cb("qst", 0, h), T.bE[:, 128:256], AF.Copy, CQ + 2048.0), 128, r=["bE1"], w=["qst0%d" % h], b=["bE"])
         for i, c in ((2, 0), (0, 2), (1, 3)):
-            s(act(cb("lst", i, h), T.bE[:, 128 * c:128 * c + 128], AF.Copy, 8192.0), 128, r=["bE%d" % c], w=["lst%d%d" % (i, h)], b=["bE"])
+            s(act(cb("lst", i, h), T.bE[:, 128 * c:128 * c + 128], AF.Copy, CP + 2048.0), 128, r=["bE%d" % c], w=["lst%d%d" % (i, h)], b=["bE"])
 
     P = 2048 // PCS
-    first, dn = {}, [0]
+    dn = [0]
 
     def tabs(t):
         x = "x%d" % t
         e = ["xe0"] if t == 0 else [x]
         late = [first[(t - 1, 1)]] if t else []
         v(ts(T["thm%d" % t][:, 0:128], T.ib[:], T[x][:, 4096:4097], OP.mult), 128, 0.5, r=["ib"] + e, w=["thm%d" % t], after=late)
-        v(ms(T["thm%d" % t][:, 128:512], 0.0), 384, 0.5, w=["thz%d" % t])
-        v(ts(T["thm%d" % t][:, 512:640], T.ib[:], T[x][:, 4097:4098], OP.mult), 128, 0.5, r=["ib"] + e, w=["thn%d" % t], after=late)
+        v(ts(T["thm%d" % t][:, 128:256], T.ib[:], T[x][:, 4097:4098], OP.mult), 128, 0.5, r=["ib"] + e, w=["thn%d" % t], after=late)
         v(ts(T["wb%d" % t][:], T.b128[:], T[x][:, 4098:4099], OP.mult), 128, 0.5, r=["b128"] + e, w=["wb%d" % t], after=late)
 
     def big(t, h):
@@ -258,7 +276,11 @@ def _plan(g, core, T, topo):
         K = lambda n, j: n + hh + "p%d" % j
         for j in range(PCS):
             sl = slice(P * j, P * j + P)
-            s(act(B["sg"][:, sl], win.indirect(off("u16l", t + 1, j)), AF.Copy), P * GATH, r=[x, "u16l%d%d" % (t + 1, h)], w=[K("sg", j)])
+            kw = dict(r=[x, "u16l%d%d" % (t + 1, h)], w=[K("sg", j)])
+            if (t, h) == (0, 0) and j:
+                v(cp(B["sg"][:, sl], win.indirect(off("u16l", t + 1, j))), P * GATH, **kw)
+            else:
+                s(act(B["sg"][:, sl], win.indirect(off("u16l", t + 1, j)), AF.Copy), P * GATH, **kw)
         for j in range(PCS):
             sl = slice(P * j, P * j + P)
             s(act(B["lg"][:, sl], win.indirect(off("u16l", t + 2, j)), AF.Copy), P * GATH, r=[x, "u16l%d%d" % (t + 2, h)], w=[K("lg", j)])
@@ -273,9 +295,9 @@ def _plan(g, core, T, topo):
             v(lambda a=B["mx"][:, sl], b=B["lg"][:, sl]: g.vector.tensor_tensor_scan(a, T.msk[:], b, 0.0, OP.mult, OP.max), P, 0.5,
               r=["msk", K("lg", j)], w=[K("mx", j)])
         mo = "mo%d%d" % (t, h)
-        s(act(cb("mo", t, h), B["mx"][:, 15::16], AF.Copy), 128, r=[K("mx", j) for j in range(PCS)], w=[mo])
+        v(cp(cb("mo", t, h), B["mx"][:, 15::16]), 128, 0.5, r=[K("mx", j) for j in range(PCS)], w=[mo])
         d2 = dst(2)
-        send("rm%d%d" % (t, h), cb("mi", t, h), cb("mo", t, h), d2, topo.engines(core, d2)[4:8], mo, 4.0, "mi%d%d" % (t, h))
+        send("rm%d%d" % (t, h), cb("mi", t, h), cb("mo", t, h), d2, topo.engines(core, d2)[1:8:2], mo, LAT, "mi%d%d" % (t, h))
         for j in range(PCS):
             sl = slice(P * j, P * j + P)
             v(tt(B["dd"][:, sl], win.indirect(off("u16q", t, j)), B["sg"][:, sl], OP.subtract), P * GATH,
@@ -302,6 +324,13 @@ def _plan(g, core, T, topo):
         e = "e%d%d" % (t, h)
         for j in range(4):
             d = "d%d" % ((dn[0] + j) % 3)
+            if (t, h, j) in OMAX:
+                mm([MM(T[d][:, 0:128], T.ib[:], T[e][:, 0:128], True, True)], 128, r=[e, "ib"], w=[d], b=[d])
+                for i in range(4):
+                    k = 4 * j + i
+                    v(tt(B["ao"][:, 128 * k:128 * k + 128], B["lg"][:, k::16], T[d][:, 0:128], OP.max), 128,
+                      r=[K("lg", jj) for jj in range(PCS)] + [d], w=["ao%sp%dk%d" % (hh, j, i)], b=[d])
+                continue
             fn = []
             for i in range(4):
                 o_ = T[d][:, 128 * i:128 * i + 128]
@@ -313,7 +342,7 @@ def _plan(g, core, T, topo):
     def logic(t, h):
         hh, n = str(h), 128
         tm = t % 4
-        B = {nm: T[nm + hh] for nm in ("da", "dd", "ra", "rd", "ab", "ac", "ao")}
+        B = {nm: T[nm + hh] for nm in ("lg", "da", "dd", "ra", "rd", "ab", "ac", "ao")}
         A, Bb, D, E = T["bA" + hh], T.bB, T.bD, T.bE
         half[0] = hh
         k_ = lambda nm: nm + hh
@@ -331,8 +360,18 @@ def _plan(g, core, T, topo):
             fn = []
             for k in range(16):
                 lt = B[nm][:, 128 * k:128 * k + 128] if nm == "ao" else B[nm][:, k::16]
-                fn.append(MM(A[:, a + k:b:16], lt, T.fun[:, FUN[nm][0]:FUN[nm][1]], False, False))
-            mm(fn, 64 * len(fn), r=pcs(nm) + FK, a=["A"], b=["bA"])
+                if nm == "ao" and (t, h, k // 4) in OMAX:
+                    fn.append(MM(A[:, a + k:b:16], lt, T.fun[:, 80:88], False, False))
+                    mm([MM(A[:, a + k:b:16], B["lg"][:, k::16], T.fun[:, 88:96], False, False),
+                        MM(A[:, a + k:b:16], T[e][:, 0:128], T.fun[:, 88:96], False, False)], 128, r=pcs("lg") + [e] + FK, a=["A"], b=["bA"])
+                else:
+                    fn.append(MM(A[:, a + k:b:16], lt, T.fun[:, FUN[nm][0]:FUN[nm][1]], False, False))
+            rr = pcs(nm)
+            if nm == "ao":
+                for j in range(4):
+                    if (t, h, j) in OMAX:
+                        rr += ["ao%sp%dk%d" % (hh, j, i) for i in range(4)]
+            mm(fn, 64 * len(fn), r=rr + FK, a=["A"], b=["bA"])
 
         sums("ra", 256, 384)
         sums("da", 256, 384)
@@ -341,7 +380,7 @@ def _plan(g, core, T, topo):
         sums("ab", 0, 384)
         sums("ac", 128, 384)
         sums("ao", 384, 512)
-        mm([MM(A[:], T.one[:], T["thm%d" % tm][:, 128:640], False, True)], 512, r=["one", "thn%d" % tm, "thz%d" % tm], w=["A"], b=["bA"])
+        mm([MM(A[:, 384:512], T.one[:], T["thm%d" % tm][:, 128:256], False, True)], 128, r=["one", "thn%d" % tm], w=["A"], b=["bA"])
         X2, X1, XF, X3 = [A[:, 128 * i:128 * i + 128] for i in range(4)]
         mm([MM(D[:, 0:128], T[e][:, 0:128], T["wb%d" % tm][:], True, True)], 128, r=[e, "wb%d" % tm], w=["Du"], b=["bD"])
         if h == 0:
@@ -350,39 +389,37 @@ def _plan(g, core, T, topo):
             else:
                 v(ts(T.ka[:], T.k37[:], T["e%d1" % t][:, 128:129], OP.add), n, r=["k37", "e%d1" % t], w=["ka"])
         lh, qo = cb("lh", t, h), cb("qst", t, h)
-        PL, PY, PLm, PLQ = [Bb[:, 128 * i:128 * i + 128] for i in range(4)]
+        PL, PY, PLQ = [Bb[:, 128 * i:128 * i + 128] for i in range(3)]
         mm([MM(PL, one_row, T.rowb[0:1, 0:128], True, False), MM(PL, T.i16[:], lh, False, True),
-            MM(PY, one_row, T.rowb[0:1, 0:128], True, False), MM(PY, T.i16[:], lh, False, False), MM(PY, T.i16[:], T.ka[:], False, True),
-            MM(PLm, one_row, T.rowb[0:1, 128:256], True, False), MM(PLm, T.i16[:], lh, False, True),
-            MM(PLQ, T.i16[:], lh, True, False), MM(PLQ, T.n16[:], cb("qh", t, h), False, True)], 9 * 128,
+            MM(PY, one_row, T.rowb[0:1, 128:256], True, False), MM(PY, T.i16[:], lh, False, False), MM(PY, T.i16[:], T.ka[:], False, True),
+            MM(PLQ, T.i16[:], lh, True, False), MM(PLQ, T.n16[:], cb("qh", t, h), False, True)], 7 * 128,
            r=["one", "i16", "n16", "lh%d%d" % (t, h), "qh%d%d" % (t, h), "ka"] + CB_, w=["B"], b=["bB"])
         v(cp(it("ui"), D[:, 0:128]), n, r=["Du"], w=[k_("ui")], b=["bD"])
         v(ts(it("uj"), it("ui"), 4095, OP.bitwise_and), n, r=[k_("ui")], w=[k_("uj")])
         v(tt(it("z"), it("uj"), PL, OP.mult), n, r=[k_("uj"), "B"], w=[k_("z")], b=["bB"])
         v(ts(it("zs"), it("z"), 5, OP.arith_shift_right), n, r=[k_("z")], w=[k_("zs")])
         v(tt(it("y"), it("zs"), PY, OP.add), n, r=[k_("zs"), "B"], w=[k_("y")], b=["bB"])
-        v(ts(it("ch"), it("y"), 4095, OP.bitwise_and), n, r=[k_("y")], w=[k_("ch")])
         ms_, fz = T.msk[:, 0:128], T["fz" + hh]
         v(lambda: g.vector.tensor_tensor_scan(ft("sc"), ms_, XF, 0.0, OP.mult, OP.add), n, r=["A", "msk"], w=[k_("sc")], b=["bA"])
-        v(ts(fz[:, 0::16], T.ftmp[:, FTMP.index("sc") * 256 + 128 * h + 15:FTMP.index("sc") * 256 + 128 * h + 128:16], 0.0, OP.is_lt), 8,
+        v(ts(fz[:, 0::16], T.ftmp[:, FTMP.index("sc") * 256 + 128 * h + 15:FTMP.index("sc") * 256 + 128 * h + 128:16], 0.0, OP.is_ge, GATE, OP.mult), 8,
           r=[k_("sc"), "fz0" + hh], w=[k_("fz")])
         v(lambda: g.vector.tensor_tensor_scan(fl[:], ms_, fz[:], 0.0, OP.mult, OP.add), n, 0.5, r=["msk", k_("fz")], w=[k_("fl") + "a"])
-        v(ts(T["gf" + hh][:], fl[:], 65536.0, OP.mult, 65536.0, OP.subtract), n, 0.5, r=[k_("fl") + "a"], w=[k_("gf")])
         FL = [k_("fl") + "a"]
-        mm([MM(D[:, 256:384], T.ib[:], T[e][:, 0:128], True, False), MM(D[:, 256:384], T.nib[:], cb("mi", t, h), False, True),
-            MM(D[:, 384:512], T.hib[:], T[e][:, 0:128], True, False), MM(D[:, 384:512], T.hib[:], cb("mi", t, h), False, False),
-            MM(D[:, 384:512], one_row, T.rowq[0:1, :], False, False), MM(D[:, 384:512], fl[:], T.im512[:], False, True),
-            MM(D[:, 128:256], fl[:], T.i1024[:], True, True)], 7 * 128,
-           r=FL + [e, mi, "ib", "nib", "hib", "one", "rowq0", "im512", "i1024"], w=["De"], b=["bD"])
-        s(act(ft("absd"), D[:, 256:384], AF.Abs), n, r=["De"], w=[k_("absd")], b=["bD"])
-        v(ts(ft("t2"), D[:, 384:512], MAGIC, OP.add, MAGIC, OP.subtract), n, r=["De"], w=[k_("t2")], b=["bD"])
-        v(tt(E[:, 0:128], ft("absd"), D[:, 128:256], OP.min), n, r=["De", k_("absd")], w=["bE0"], b=["bD", "bE"])
-        v(tt(T[eo][:, 0:128], ft("t2"), E[:, 0:128], OP.max), n, r=[k_("t2"), "bE0"], w=[eo], b=["bE"])
+        mm([MM(D[:, 256:384], T.ib[:], T[e][:, 0:128], True, False), MM(D[:, 256:384], T.nib[:], cb("mi", t, h), False, True)], 256,
+           r=[e, mi, "ib", "nib"], w=["Dd"], b=["bD"])
+        absd = T["absd" + hh][:]
+        s(act(absd, D[:, 256:384], AF.Abs), n, r=["Dd"], w=[k_("absd")], b=["bD"])
+        mm([MM(D[:, 384:512], T.ib[:], T[e][:, 0:128], True, False), MM(D[:, 384:512], T.ib[:], cb("mi", t, h), False, False),
+            MM(D[:, 384:512], fl[:], T.i1024[:], False, True),
+            MM(D[:, 128:256], fl[:], T.im512[:], True, False), MM(D[:, 128:256], T.ib[:], absd, False, True)], 5 * 128,
+           r=FL + [e, mi, k_("absd"), "ib", "im512", "i1024"], w=["De"], b=["bD"])
+        v(ts(it("t2"), D[:, 384:512], 0.5, OP.mult, 512.25, OP.subtract), n, r=["De"], w=[k_("t2")], b=["bD"])
+        v(tt(T[eo][:, 0:128], it("t2"), D[:, 128:256], OP.max), n, r=[k_("t2"), "De"], w=[eo], b=["bD"])
         if t < V - 1:
             if h == 1:
-                mm([MM(D[:, 0:1], T.one[:], T["fl%d" % a][:, 16 * q:16 * q + 1], (a, q) == (0, 0), (a, q) == (1, 7)) for a in range(2) for q in range(8)],
-                   1024, r=FL + ["fl0a", "one"], w=["Du"], b=["bD"])
-                v(cp(T.acol[:, 0:1], D[:, 0:1]), 1, r=["Du"], w=["ac0"], b=["bD"])
+                mm([MM(D[:, 0:8], T.onec[:], T["fl%d" % a][:, 0::16], a == 0, a == 1) for a in range(2)], 128, r=FL + ["fl0a", "onec"], w=["Du"], b=["bD"])
+                v(lambda: g.vector.tensor_reduce(T.cnt[:, 0:1], D[:, 0:8], AX.X, OP.add), 8, r=["Du"], w=["cnt"], b=["bD"])
+                v(ts(T.acol[:, 0:1], T.cnt[:, 0:1], -1.0, OP.mult), 1, r=["cnt"], w=["ac0"])
                 v(ts(T.acol[:, 1:2], T.acol[:, 0:1], 31, OP.bitwise_and), 1, r=["ac0"], w=["ac1"])
                 v(ms(T[eo][:, 128:144], 0.0), 16, w=[eo + "A"])
                 v(cp(T[eo][:, 128:129], T.acol[:, 1:2]), 1, r=["ac1"], w=[eo + "A"])
@@ -390,22 +427,22 @@ def _plan(g, core, T, topo):
                 v(ms(T[eo][:, 128:144], 0.0), 16, w=[eo + "A"])
             d1 = dst(-1)
             en = "e%d%d" % (t + 1, h)
-            send("re%d%d" % (t + 1, h), T[en][:], T[eo][:], d1, topo.engines(core, d1)[4:8], eo, 4.0, en, after=[last_w[eo + "A"]])
+            send("re%d%d" % (t + 1, h), T[en][:], T[eo][:], d1, topo.engines(core, d1)[1:8:2], eo, LAT, en, after=[last_w[eo + "A"]])
         else:
             op("Y", 0.1, [lambda: g.sync.dma_start(T.ye[:, 128 * h:128 * h + 128], T[eo][:, 0:128])], r=[eo], sig=("d_ye%d" % h, 16), lat=2.0)
         pst = cb("lst", t, h)
-        v(tt(ft("m3"), it("ch"), X3, OP.min), n, r=[k_("ch"), "A"], w=[k_("m3")], b=["bA"])
-        v(tt(ft("r3"), ft("m3"), PLm, OP.max), n, r=[k_("m3"), "B"], w=[k_("r3")], b=["bB"])
+        v(tt(ft("m3"), it("y"), X3, OP.min), n, r=[k_("y"), "A"], w=[k_("m3")], b=["bA"])
+        v(tt(ft("r3"), ft("m3"), PL, OP.max), n, r=[k_("m3"), "B"], w=[k_("r3")], b=["bB"])
         v(tt(E[:, 0:128], qo, X2, OP.min), n, r=["qst%d%d" % (t, h), "A"], w=["bE0"], b=["bA", "bE"])
         v(tt(E[:, 128:256], pst, X1, OP.min), n, r=["lst%d%d" % (t, h), "A"], w=["bE1"], b=["bA", "bE"])
-        v(tt(ft("m1"), T["gf" + hh][:], E[:, 128:256], OP.add), n, r=[k_("gf"), "bE1"], w=[k_("m1")], b=["bE"])
+        v(tt(ft("m1"), E[:, 128:256], fl[:], OP.subtract), n, r=FL + ["bE1"], w=[k_("m1")], b=["bE"])
         v(tt(E[:, 0:128], ft("r3"), E[:, 0:128], OP.max), n, r=[k_("r3"), "bE0"], w=["bE0"], b=["bE"])
         v(tt(it("r1"), ft("m1"), E[:, 0:128], OP.max), n, r=[k_("m1"), "bE0"], w=[k_("r1")], b=["bE"])
         nw = it("nw")
         v(ts(nw, it("r1"), 4095, OP.bitwise_and), n, r=[k_("r1")], w=[k_("nw")])
         v(ts(cb("lh", t + 1, h), nw, 2048.0, OP.subtract), n, r=[k_("nw")], w=["lh%d%d" % (t + 1, h)])
         if t + 3 < 5:
-            v(ts(cb("lst", t + 3, h), nw, 8192.0, OP.add), n, r=[k_("nw")], w=["lst%d%d" % (t + 3, h)])
+            v(ts(cb("lst", t + 3, h), nw, CP, OP.add), n, r=[k_("nw")], w=["lst%d%d" % (t + 3, h)])
         qn = cb("qst", t + 1, h)
         v(tt(ft("ne"), nw, PL, OP.not_equal), n, r=[k_("nw"), "B"], w=[k_("ne")], b=["bB"])
         v(tt(E[:, 128:256], ft("ne"), PLQ, OP.mult), n, r=[k_("ne"), "B"], w=["bE1"], b=["bB", "bE"])
@@ -413,7 +450,7 @@ def _plan(g, core, T, topo):
         mm([MM(E[:, 256:384], cb("lh", t + 1, h), T.i16[:], True, True)], 128, r=["i16", "lh%d%d" % (t + 1, h)], w=["bE2"], b=["bE"])
         if t < V - 1:
             v(ts(cb("u16l", t + 3, h), E[:, 256:384], 2048.0, OP.add), n, r=["bE2"], w=["u16l%d%d" % (t + 3, h)], b=["bE"])
-        v(ts(cb("qh", t + 1, h), qn, 6144.0, OP.subtract), n, r=["qst%d%d" % (t + 1, h)], w=["qh%d%d" % (t + 1, h)])
+        v(ts(cb("qh", t + 1, h), qn, CQ + 2048.0, OP.subtract), n, r=["qst%d%d" % (t + 1, h)], w=["qh%d%d" % (t + 1, h)])
         mm([MM(E[:, 384:512], cb("qh", t + 1, h), T.i16[:], True, True)], 128, r=["i16", "qh%d%d" % (t + 1, h)], w=["bE3"], b=["bE"])
         if t < V - 1:
             v(ts(cb("u16q", t + 1, h), E[:, 384:512], 2048.0, OP.add), n, r=["bE3"], w=["u16q%d%d" % (t + 1, h)], b=["bE"])
@@ -433,55 +470,69 @@ def _plan(g, core, T, topo):
         for h in range(H2):
             big(t, h)
             logic(t, h)
-        if t == 0:
+        if t == 1:
             send_table(2, [])
+        if t == 2:
             send_table(3, [first[(0, 1)]])
     return ops
 
 
 def _order(ops):
     n = len(ops)
+    pred = [sorted(o["d"]) for o in ops]
     succ = [[] for _ in range(n)]
-    for o in ops:
-        for d in o["d"]:
-            succ[d].append(o["i"])
-    prio = [0.0] * n
-    for o in reversed(ops):
-        m = 0.0
-        for k in succ[o["i"]]:
-            if prio[k] > m:
-                m = prio[k]
-        prio[o["i"]] = m + o["c"] + o["lat"] + 0.05
-    left = [len(o["d"]) for o in ops]
-    ready_t = [0.0] * n
-    free, ready, order = {}, {}, {}
-    for o in ops:
-        if not left[o["i"]]:
-            ready.setdefault(o["q"], []).append(o["i"])
-    done = 0
-    while done < n:
-        best = None
-        for q, lst in ready.items():
-            f = free.get(q, 0.0)
-            for i in lst:
-                st = max(f, ready_t[i])
-                key = (st, -prio[i])
-                if best is None or key < best[0]:
-                    best = (key, q, i)
-        (st, _), q, i = best
-        o = ops[i]
-        ready[q].remove(i)
-        order.setdefault(q, []).append(o)
-        fin = st + o["c"]
-        if q != "R":
-            free[q] = fin
-        for k in succ[i]:
-            ready_t[k] = max(ready_t[k], fin + o["lat"] + 0.08)
-            left[k] -= 1
-            if not left[k]:
-                ready.setdefault(ops[k]["q"], []).append(k)
-        o["st"] = st
-        done += 1
+    for i in range(n):
+        for d in pred[i]:
+            succ[d].append(i)
+    q, c, lat = [o["q"] for o in ops], [o["c"] for o in ops], [o["lat"] for o in ops]
+
+    def list_pass(before, after, prio, forward):
+        left = [len(b) for b in before]
+        ready_t = [0.0 if forward or after[i] else lat[i] for i in range(n)]
+        start, free, ready, seq = [0.0] * n, {}, {}, []
+        for i in range(n):
+            if not left[i]:
+                ready.setdefault(q[i], []).append(i)
+        while len(seq) < n:
+            best = None
+            for qq, lst in ready.items():
+                f = free.get(qq, 0.0)
+                for i in lst:
+                    key = (max(f, ready_t[i]), -prio[i], i)
+                    if best is None or key < best:
+                        best = key
+            st, _, i = best
+            ready[q[i]].remove(i)
+            seq.append(i)
+            start[i] = st
+            fin = st + c[i]
+            if q[i] != "R":
+                free[q[i]] = fin
+            for k in after[i]:
+                ready_t[k] = max(ready_t[k], fin + lat[i if forward else k] + WAKE)
+                left[k] -= 1
+                if not left[k]:
+                    ready.setdefault(q[k], []).append(k)
+        return start, seq
+
+    base = [0.0] * n
+    for i in reversed(range(n)):
+        base[i] = max([base[k] for k in succ[i]] + [0.0]) + c[i] + lat[i] + WAKE
+    rs = np.random.RandomState(SEED)
+    best = None
+    for trial in range(TRIES):
+        prio = [float(p + (SPREAD * x if trial else 0.0)) for p, x in zip(base, rs.random_sample(n))]
+        for turn in range(TURNS):
+            start, seq = list_pass(pred, succ, prio, True)
+            span = max(start[i] + c[i] + lat[i] for i in range(n))
+            if best is None or span < best[0] - 1e-9:
+                best = (span, start, seq)
+            back, _ = list_pass(succ, pred, [start[i] + c[i] for i in range(n)], False)
+            prio = [back[i] + c[i] for i in range(n)]
+    order = {}
+    for i in best[2]:
+        ops[i]["st"] = best[1][i]
+        order.setdefault(q[i], []).append(ops[i])
     return order
 
 

import numpy as np
from concourse.mybir import AluOpType as OP, ActivationFunctionType as AF, AxisListType as AX

V, H2 = 5, 2
PCS = 2
PE_NS, CY_NS, GATH = 0.4167, 0.83, 1.5
LAT, WAKE = 5.0, 0.08
SPREAD, SEED, TRIES, TURNS = 2.0, 849, 6, 6
SC = 2.0 ** 23
CF, CQ, CP = 8192.0, 2.0 ** 20, 2.0 ** 21
GATE = 2.0 ** 22
OMAX = set()

SCRATCH, SEMAPHORES = {}, ["sT", "sV", "sS", "sG", "lsem"]


def _buf(name, cols, dtype, where="sbuf"):
    SCRATCH[name] = (where, [128, cols], dtype)


for _n in ("d0", "d1", "d2", "bA0", "bA1", "bB", "bD", "bE"):
    _buf(_n, 512, "float32", "psum")
for _t in range(4):
    _buf("x%d" % _t, 4096 + 16, "bfloat16")
    _buf("thm%d" % _t, 256, "bfloat16")
    _buf("wb%d" % _t, 128, "bfloat16")
for _h in range(2):
    for _n in ("sg", "lg", "da", "dd", "ra", "rd", "ab", "ac", "ao", "mx"):
        _buf(_n + str(_h), 2048, "bfloat16")
    for _n in ("fl", "fz", "absd"):
        _buf(_n + str(_h), 128, "bfloat16")
ITMP, FTMP = ("ui", "uj", "z", "zs", "y", "r1", "nw", "t2"), ("m3", "r3", "m1", "ne", "sc")
_buf("itmp", len(ITMP) * 256, "int32")
_buf("ftmp", len(FTMP) * 256, "float32")
_buf("mo", V * 256, "bfloat16")
_buf("mi", V * 256, "bfloat16")
_buf("u16l", 7 * 256, "uint16")
_buf("u16q", 5 * 256, "uint16")
_buf("lst", 5 * 256, "float32")
_buf("lh", 6 * 256, "float16")
_buf("qst", 6 * 256, "float32")
_buf("qh", 6 * 256, "float16")
_buf("outs", 4 * 256, "float32")
for _t in range(V + 1):
    for _h in range(2):
        _buf("e%d%d" % (_t, _h), 144, "bfloat16")
        if _t < V:
            _buf("eo%d%d" % (_t, _h), 144, "bfloat16")
            SEMAPHORES.append("rm%d%d" % (_t, _h))
            if _t:
                SEMAPHORES.append("re%d%d" % (_t, _h))
SEMAPHORES += ["rx1", "rx2", "rx3"]
for _n in ("pl", "sl", "ll", "ql"):
    _buf("i_" + _n, 256, "int32")
    _buf("f_" + _n, 256, "float16")
_buf("i_tw", 2, "int32")
_buf("i_th", 2, "int32")
_buf("ka", 128, "float16")
_buf("k37", 128, "float32")
_buf("acol", 2, "int32")
_buf("cnt", 1, "float32")
_buf("onec", 128, "bfloat16")
_buf("one32", 128, "float32")
_buf("i32", 128, "float32")
_buf("i16", 128, "float16")
_buf("n16", 128, "float16")
for _n in ("one", "ib", "nib", "i1024", "im512", "bt", "b128"):
    _buf(_n, 128, "bfloat16")
_buf("msk", 2048 // PCS, "bfloat16")
_buf("mskk", 2048 // PCS, "bfloat16")
_buf("fun", 96, "bfloat16")
_buf("rowb", 256, "bfloat16")
_buf("rowlo", 512, "bfloat16")
LOADS = ["sl", "xt", "pl", "th", "wt", "ll", "ql", "ed0", "ed1"]
STORES = ["%s%d" % (_n, _h) for _n in ("yp", "ys", "yl", "yq", "ye") for _h in range(2)]
SEMAPHORES += ["d_" + _n for _n in LOADS + STORES]


class _Bank(dict):
    pass


def _plan(g, core, T, topo):
    rank, N = T.rank_of(core), len(T.cores)
    ops, last_w, readers, accs, banks, half = [], {}, {}, {}, {}, ["0"]

    def op(q, cost, fns, r=(), w=(), a=(), b=(), sig=None, lat=0.0, after=()):
        o = {"q": q, "c": cost, "f": fns, "d": {}, "sig": sig, "lat": lat, "i": len(ops), "n": (list(w) + list(a) + list(r) + ["?"])[0]}
        for x in after:
            o["d"][x["i"]] = 1
        r, w, a, b = [[k + half[0] if k in ("A", "A1", "bA") else k for k in ks] for ks in (r, w, a, b)]
        for k in r:
            for x in [last_w.get(k)] + accs.get(k, []):
                if x is not None:
                    o["d"][x["i"]] = 1
        for k in a:
            if last_w.get(k) is not None:
                o["d"][last_w[k]["i"]] = 1
            for x in readers.get(k, []):
                o["d"][x["i"]] = 1
        for k in w:
            for x in [last_w.get(k)] + accs.get(k, []) + readers.get(k, []):
                if x is not None:
                    o["d"][x["i"]] = 1
        for k in r:
            readers.setdefault(k, []).append(o)
        for k in a:
            accs.setdefault(k, []).append(o)
        for k in w:
            last_w[k], accs[k], readers[k] = o, [], []
        for k in b:
            bk = banks.setdefault(k, {"q": None, "cur": [], "prev": []})
            if bk["q"] != q:
                bk["q"], bk["prev"], bk["cur"] = q, bk["cur"], []
            for x in bk["prev"]:
                o["d"][x["i"]] = 1
            bk["cur"].append(o)
        o["d"].pop(o["i"], None)
        ops.append(o)
        return o

    def vec(n, cyc=1.0):
        return max(64.0, n * cyc) * CY_NS / 1000

    def mm(fns, cyc, **kw):
        return op("T", cyc * PE_NS / 1000, fns, **kw)

    def MM(out, lhsT, rhs, start, stop):
        return lambda: g.tensor.matmul(out, lhsT, rhs, start, stop)

    def v(fn, n, cyc=1.0, **kw):
        return op("V", vec(n, cyc), [fn], **kw)

    def s(fn, n, **kw):
        return op("S", vec(n), [fn], **kw)

    def tt(out, a, b, o):
        return lambda: g.vector.tensor_tensor(out, a, b, o)

    def ts(out, a, s1, o1, s2=None, o2=None):
        if o2 is None:
            return lambda: g.vector.tensor_scalar(out, a, s1, None, o1)
        return lambda: g.vector.tensor_scalar(out, a, s1, s2, o1, o2)

    def cp(out, a):
        return lambda: g.vector.tensor_copy(out, a)

    def act(out, a, f, bias=0.0, scale=1.0):
        return lambda: g.scalar.activation(out, a, f, bias=bias, scale=scale)

    def load(name, out, in_, key):
        return op("Y", 0.1, [lambda: g.sync.dma_start(out, in_)], w=[key], sig=("d_" + name, 16), lat=4.0 if name == "xt" else 2.2)

    def send(name, out, in_, dst, eng, key, lat, rkey, after=()):
        eng = [e for e in eng]
        m = sum(1 << e for e in eng)
        rid, pid, _ = topo.addr(dst)
        so = op("G", 1.3, [lambda: g.remote_dma(out, in_, T.sem[name], T.sem["lsem"], pid, rid, m)], r=[key], sig=("send", len(eng)), after=after)
        op("R", 0.0, [], w=[rkey], sig=(name, len(eng)), after=[so], lat=lat)
        return so

    def dst(k):
        return T.cores[(rank + k) % N]

    def cb(name, i, h, n=128):
        c = i * 256 + h * 128
        return T[name][:, c:c + n]

    load("sl", T.i_sl[:], T.sl[:], "i_sl")
    load("xt", T.x0[:, 0:4096], T.xt[:], "x0")
    load("pl", T.i_pl[:], T.pl[:], "i_pl")
    load("th", T.i_tw[:, 0:1], T.th[:], "i_th")
    load("wt", T.i_tw[:, 1:2], T.wt[:], "i_wt")
    load("ll", T.i_ll[:], T.ll[:], "i_ll")
    load("ql", T.i_ql[:], T.ql[:], "i_ql")
    load("ed0", T.e00[:, 0:128], T.ed[:, 0:128], "e00")
    load("ed1", T.e01[:, 0:128], T.ed[:, 128:256], "e01")
    ms = lambda ap, c: (lambda: g.vector.memset(ap, c))
    v(ms(T.one32[:], 1.0), 128, w=["one32"])
    v(ms(T.one[:], 1.0), 128, 0.5, w=["one"])
    v(ms(T.onec[:], 1.0 / GATE), 128, 0.5, w=["onec"])
    gq = lambda fn, n, **kw: op("G", 0.2 + n * 2 * CY_NS / 1000, [fn], **kw)
    gq(lambda: g.affine_select(T.i32[:], T.one32[:], [[-1, 128]], OP.is_equal, 0.0, 0, 1), 128, r=["one32"], w=["i32"])
    gq(lambda: g.affine_select(T.bt[:], T.one[:], [[-16, 8], [0, 16]], OP.is_ge, 0.0, 0, 1), 128, r=["one"], w=["bt"])
    gq(lambda: g.affine_select(T.b128[:], T.bt[:], [[16, 8], [0, 16]], OP.is_ge, 0.0, 15, -1), 128, r=["bt"], w=["b128"])
    gq(lambda: g.iota(T.mskk[:], [[0, 128 // PCS], [1, 16]], 0, 0, allow_small_or_imprecise_dtypes=True), 2048 // PCS, w=["mskk"])
    gq(lambda: g.iota(T.k37[:], [[0, 8], [37, 16]], 0, 0, allow_small_or_imprecise_dtypes=True), 128, w=["k37"])
    for nm, c in (("ib", 1.0), ("nib", -1.0), ("i1024", 1024.0 / GATE), ("im512", -512.0 / GATE), ("i16", 1.0), ("n16", -1.0)):
        if nm in ("i16", "n16"):
            v(ts(T[nm][:], T.i32[:], c, OP.mult), 128, r=["i32"], w=[nm])
        else:
            s(act(T[nm][:], T.i32[:], AF.Copy, 0.0, c), 128, r=["i32"], w=[nm])
    v(ts(T.msk[:], T.mskk[:], 0.0, OP.is_gt), 2048 // PCS, 0.5, r=["mskk"], w=["msk"])
    FUN = {"ab": (0, 24), "ac": (24, 40), "ra": (40, 48), "da": (48, 56), "rd": (56, 64), "dd": (64, 72), "ao": (72, 80)}
    for i, c in enumerate((SC, SC, -2.0, -SC, 2.0, -2.0, 1.0, -2 * SC, SC, SC, 2 * SC, -SC)):
        s(act(T.fun[:, 8 * i:8 * i + 8], T.b128[:, 0::16], AF.Copy, 0.0, c), 8, r=["b128"], w=["fun%d" % i])
    for nm, a, b, c in (("rowlo", 0, 256, -SC / 2), ("rowlo", 256, 384, 0.0), ("rowlo", 384, 512, SC / 2),
                        ("rowb", 0, 128, 2048.0), ("rowb", 128, 256, 2048.0 + CF)):
        v(ms(T[nm][0:1, a:b], c), b - a, w=[nm + str(a)])
    for h in range(H2):
        v(ms(T["fz%d" % h][:], 0.0), 128, 0.5, w=["fz0%d" % h])
    CK = ["rowlo0", "rowlo256", "rowlo384"]
    CB_ = ["rowb0", "rowb128"]
    FK = ["fun%d" % i for i in range(12)]
    one_row = T.one[0:1, :]
    v(ts(T.i_th[:, 0:1], T.i_tw[:, 0:1], 4, OP.arith_shift_right), 1, r=["i_th"], w=["thh"])
    v(ts(T.i_th[:, 1:2], T.i_tw[:, 0:1], 15, OP.bitwise_and), 1, r=["i_th"], w=["thl"])
    v(ms(T.x0[:, 4096:4112], 0.0), 16, w=["xe0"])
    v(ts(T.x0[:, 4096:4097], T.i_th[:, 0:1], -SC * 16, OP.mult), 1, r=["thh"], w=["xe0"])
    v(ts(T.x0[:, 4097:4098], T.i_th[:, 1:2], -SC, OP.mult), 1, r=["thl"], w=["xe0"])
    v(cp(T.x0[:, 4098:4099], T.i_tw[:, 1:2]), 1, r=["i_wt"], w=["xe0"])
    tab_ready = [o for o in ops if o["i"] in (last_w["x0"]["i"], last_w["xe0"]["i"])]

    first = {}

    def relayed(home, t):
        c, c1, c0 = T.cores[home], T.cores[(home + 1) % N], T.cores[(home + t) % N]
        return t > 1 and topo.chip(c) != topo.chip(c0) and topo.chip(c) == topo.chip(c1)

    def send_table(t, after):
        def tab_engines(a, b):
            en = topo.engines(a, b)
            return en if len(en) >= 16 or t == 1 else en[0:8:2]

        back = (rank - t) % N
        outs = [] if relayed(back, t) else [(T.cores[back], "x0", tab_ready)]
        if relayed((rank - 1) % N, t):
            outs.append((dst(-1), "x%d" % (t - 1), []))
        for d, src, rd in outs:
            en = tab_engines(core, d)
            m = sum(1 << k for k in en)
            rid, pid, _ = topo.addr(d)
            op("G", 1.3, [lambda src=src, rid=rid, pid=pid, m=m: g.remote_dma(T["x%d" % t][:], T[src][:], T.sem["rx%d" % t], T.sem["lsem"], pid, rid, m)],
               r=[src], sig=("send", len(en)), after=rd + (after if src == "x0" else [first[(t - 2, 1)]]))
        frm = dst(1) if relayed(rank, t) else dst(t)
        op("R", 0.0, [], w=["x%d" % t], sig=("rx%d" % t, len(tab_engines(frm, core))), after=tab_ready + after, lat=16.0 if t == 1 else 30.0)

    send_table(1, [])
    for nm, i in (("sl", 1), ("pl", 0), ("ll", 2)):
        v(cp(T.u16l[:, 256 * i:256 * i + 256], T["i_" + nm][:]), 256, r=["i_" + nm], w=["u16l%d0" % i, "u16l%d1" % i])
    v(cp(T.u16q[:, 0:256], T.i_ql[:]), 256, r=["i_ql"], w=["u16q00", "u16q01"])
    for nm in ("ll", "ql", "pl", "sl"):
        v(ts(T["f_" + nm][:], T["i_" + nm][:], 2048.0, OP.subtract), 256, r=["i_" + nm], w=["f_" + nm])

    def first_page_form(h):
        hs = slice(128 * h, 128 * h + 128)
        for c, nm in enumerate(("ll", "ql", "pl", "sl")):
            mm([MM(T.bE[:, 128 * c:128 * c + 128], T["f_" + nm][:, hs], T.i16[:], True, True)], 128, r=["f_" + nm, "i16"], w=["bE%d" % c], b=["bE"])
        v(cp(cb("lh", 0, h), T.bE[:, 0:128]), 128, r=["bE0"], w=["lh0%d" % h], b=["bE"])
        v(cp(cb("qh", 0, h), T.bE[:, 128:256]), 128, r=["bE1"], w=["qh0%d" % h], b=["bE"])
        s(act(cb("qst", 0, h), T.bE[:, 128:256], AF.Copy, CQ + 2048.0), 128, r=["bE1"], w=["qst0%d" % h], b=["bE"])
        for i, c in ((2, 0), (0, 2), (1, 3)):
            s(act(cb("lst", i, h), T.bE[:, 128 * c:128 * c + 128], AF.Copy, CP + 2048.0), 128, r=["bE%d" % c], w=["lst%d%d" % (i, h)], b=["bE"])

    P = 2048 // PCS
    dn = [0]

    def tabs(t):
        x = "x%d" % t
        e = ["xe0"] if t == 0 else [x]
        late = [first[(t - 1, 1)]] if t else []
        v(ts(T["thm%d" % t][:, 0:128], T.ib[:], T[x][:, 4096:4097], OP.mult), 128, 0.5, r=["ib"] + e, w=["thm%d" % t], after=late)
        v(ts(T["thm%d" % t][:, 128:256], T.ib[:], T[x][:, 4097:4098], OP.mult), 128, 0.5, r=["ib"] + e, w=["thn%d" % t], after=late)
        v(ts(T["wb%d" % t][:], T.b128[:], T[x][:, 4098:4099], OP.mult), 128, 0.5, r=["b128"] + e, w=["wb%d" % t], after=late)

    def big(t, h):
        hh = str(h)
        x = "x%d" % (t % 4)
        win = T[x][:, 0:4096]
        B = {n: T[n + hh] for n in ("sg", "lg", "da", "dd", "ra", "rd", "ab", "ac", "ao", "mx")}

        def off(buf, i, j):
            c = i * 256 + h * 128 + j * (128 // PCS)
            return T[buf][:, c:c + 128 // PCS]

        K = lambda n, j: n + hh + "p%d" % j
        for j in range(PCS):
            sl = slice(P * j, P * j + P)
            kw = dict(r=[x, "u16l%d%d" % (t + 1, h)], w=[K("sg", j)])
            if (t, h) == (0, 0) and j:
                v(cp(B["sg"][:, sl], win.indirect(off("u16l", t + 1, j))), P * GATH, **kw)
            else:
                s(act(B["sg"][:, sl], win.indirect(off("u16l", t + 1, j)), AF.Copy), P * GATH, **kw)
        for j in range(PCS):
            sl = slice(P * j, P * j + P)
            s(act(B["lg"][:, sl], win.indirect(off("u16l", t + 2, j)), AF.Copy), P * GATH, r=[x, "u16l%d%d" % (t + 2, h)], w=[K("lg", j)])
        for j in range(PCS):
            sl = slice(P * j, P * j + P)
            o = v(tt(B["da"][:, sl], win.indirect(off("u16l", t, j)), B["sg"][:, sl], OP.subtract), P * GATH,
                  r=[x, "u16l%d%d" % (t, h), K("sg", j)], w=[K("da", j)])
            first[(t, h)] = o
            v(ts(B["ra"][:, sl], B["da"][:, sl], 0.0, OP.max), P, 0.5, r=[K("da", j)], w=[K("ra", j)])
        for j in range(PCS):
            sl = slice(P * j, P * j + P)
            v(lambda a=B["mx"][:, sl], b=B["lg"][:, sl]: g.vector.tensor_tensor_scan(a, T.msk[:], b, 0.0, OP.mult, OP.max), P, 0.5,
              r=["msk", K("lg", j)], w=[K("mx", j)])
        mo = "mo%d%d" % (t, h)
        v(cp(cb("mo", t, h), B["mx"][:, 15::16]), 128, 0.5, r=[K("mx", j) for j in range(PCS)], w=[mo])
        d2 = dst(2)
        send("rm%d%d" % (t, h), cb("mi", t, h), cb("mo", t, h), d2, topo.engines(core, d2)[1:8:2], mo, LAT, "mi%d%d" % (t, h))
        for j in range(PCS):
            sl = slice(P * j, P * j + P)
            v(tt(B["dd"][:, sl], win.indirect(off("u16q", t, j)), B["sg"][:, sl], OP.subtract), P * GATH,
              r=[x, "u16q%d%d" % (t, h), K("sg", j)], w=[K("dd", j)])
            v(ts(B["rd"][:, sl], B["dd"][:, sl], 0.0, OP.max), P, 0.5, r=[K("dd", j)], w=[K("rd", j)])
        def size_b(j):
            d, sl, gp = "d%d" % (dn[0] % 3), slice(512 * j, 512 * j + 512), 512 * j // P
            for nm, mat, st, sp in (("sg", "ib", True, False), ("lg", "nib", False, True)):
                mm([MM(T[d][:], T[mat][:], B[nm][:, sl], st, sp)], 512, r=[K(nm, gp), mat] + ([] if st else [d]), w=[d], b=[d])
            s(act(B["ab"][:, sl], T[d][:], AF.Abs), 512, r=[d], w=["ab%sp%d" % (hh, j)], b=[d])
            dn[0] += 1

        def size_c(j):
            d, sl, gp = "d%d" % (dn[0] % 3), slice(512 * j, 512 * j + 512), 512 * j // P
            for nm, mat in (("sg", "ib"), ("da", "ib"), ("lg", "nib")):
                mm([MM(T[d][:], T[mat][:], B[nm][:, sl], nm == "sg", nm == "lg")], 512, r=[K(nm, gp), mat] + ([] if nm == "sg" else [d]), w=[d], b=[d])
            s(act(B["ac"][:, sl], T[d][:], AF.Abs), 512, r=[d], w=["ac%sp%d" % (hh, j)], b=[d])
            dn[0] += 1

        for j in range(4):
            size_b(j)
        for j in range(4):
            size_c(j)
        e = "e%d%d" % (t, h)
        for j in range(4):
            d = "d%d" % ((dn[0] + j) % 3)
            if (t, h, j) in OMAX:
                mm([MM(T[d][:, 0:128], T.ib[:], T[e][:, 0:128], True, True)], 128, r=[e, "ib"], w=[d], b=[d])
                for i in range(4):
                    k = 4 * j + i
                    v(tt(B["ao"][:, 128 * k:128 * k + 128], B["lg"][:, k::16], T[d][:, 0:128], OP.max), 128,
                      r=[K("lg", jj) for jj in range(PCS)] + [d], w=["ao%sp%dk%d" % (hh, j, i)], b=[d])
                continue
            fn = []
            for i in range(4):
                o_ = T[d][:, 128 * i:128 * i + 128]
                fn += [MM(o_, T.ib[:], B["lg"][:, 4 * j + i::16], True, False), MM(o_, T.nib[:], T[e][:, 0:128], False, True)]
            mm(fn, 1024, r=[K("lg", jj) for jj in range(PCS)] + [e, "ib", "nib"], w=[d], b=[d])
            s(act(B["ao"][:, 512 * j:512 * j + 512], T[d][:], AF.Abs), 512, r=[d], w=["ao%sp%d" % (hh, j)], b=[d])
        dn[0] += 4

    def logic(t, h):
        hh, n = str(h), 128
        tm = t % 4
        B = {nm: T[nm + hh] for nm in ("lg", "da", "dd", "ra", "rd", "ab", "ac", "ao")}
        A, Bb, D, E = T["bA" + hh], T.bB, T.bD, T.bE
        half[0] = hh
        k_ = lambda nm: nm + hh
        pcs = lambda nm: [nm + hh + "p%d" % j for j in range(4 if nm[0] == "a" else PCS)]
        fl = T["fl" + hh]
        it = lambda nm: cb("itmp", ITMP.index(nm), h)
        ft = lambda nm: cb("ftmp", FTMP.index(nm), h)
        e, eo, mi = "e%d%d" % (t, h), "eo%d%d" % (t, h), "mi%d%d" % (t, h)
        if t == 0:
            first_page_form(h)
        mm([MM(A[:], one_row, T.rowlo[0:1, :], True, False)], 512, r=["one"] + CK, w=["A"], b=["bA"])
        mm([MM(A[:, 384:512], T.one[:], T["thm%d" % tm][:, 0:128], False, False)], 128, r=["one", "thm%d" % tm], a=["A"], b=["bA"])

        def sums(nm, a, b):
            fn = []
            for k in range(16):
                lt = B[nm][:, 128 * k:128 * k + 128] if nm == "ao" else B[nm][:, k::16]
                if nm == "ao" and (t, h, k // 4) in OMAX:
                    fn.append(MM(A[:, a + k:b:16], lt, T.fun[:, 80:88], False, False))
                    mm([MM(A[:, a + k:b:16], B["lg"][:, k::16], T.fun[:, 88:96], False, False),
                        MM(A[:, a + k:b:16], T[e][:, 0:128], T.fun[:, 88:96], False, False)], 128, r=pcs("lg") + [e] + FK, a=["A"], b=["bA"])
                else:
                    fn.append(MM(A[:, a + k:b:16], lt, T.fun[:, FUN[nm][0]:FUN[nm][1]], False, False))
            rr = pcs(nm)
            if nm == "ao":
                for j in range(4):
                    if (t, h, j) in OMAX:
                        rr += ["ao%sp%dk%d" % (hh, j, i) for i in range(4)]
            mm(fn, 64 * len(fn), r=rr + FK, a=["A"], b=["bA"])

        sums("ra", 256, 384)
        sums("da", 256, 384)
        sums("rd", 0, 128)
        sums("dd", 0, 128)
        sums("ab", 0, 384)
        sums("ac", 128, 384)
        sums("ao", 384, 512)
        mm([MM(A[:, 384:512], T.one[:], T["thm%d" % tm][:, 128:256], False, True)], 128, r=["one", "thn%d" % tm], w=["A"], b=["bA"])
        X2, X1, XF, X3 = [A[:, 128 * i:128 * i + 128] for i in range(4)]
        mm([MM(D[:, 0:128], T[e][:, 0:128], T["wb%d" % tm][:], True, True)], 128, r=[e, "wb%d" % tm], w=["Du"], b=["bD"])
        if h == 0:
            if t == 0:
                v(cp(T.ka[:], T.k37[:]), n, r=["k37"], w=["ka"])
            else:
                v(ts(T.ka[:], T.k37[:], T["e%d1" % t][:, 128:129], OP.add), n, r=["k37", "e%d1" % t], w=["ka"])
        lh, qo = cb("lh", t, h), cb("qst", t, h)
        PL, PY, PLQ = [Bb[:, 128 * i:128 * i + 128] for i in range(3)]
        mm([MM(PL, one_row, T.rowb[0:1, 0:128], True, False), MM(PL, T.i16[:], lh, False, True),
            MM(PY, one_row, T.rowb[0:1, 128:256], True, False), MM(PY, T.i16[:], lh, False, False), MM(PY, T.i16[:], T.ka[:], False, True),
            MM(PLQ, T.i16[:], lh, True, False), MM(PLQ, T.n16[:], cb("qh", t, h), False, True)], 7 * 128,
           r=["one", "i16", "n16", "lh%d%d" % (t, h), "qh%d%d" % (t, h), "ka"] + CB_, w=["B"], b=["bB"])
        v(cp(it("ui"), D[:, 0:128]), n, r=["Du"], w=[k_("ui")], b=["bD"])
        v(ts(it("uj"), it("ui"), 4095, OP.bitwise_and), n, r=[k_("ui")], w=[k_("uj")])
        v(tt(it("z"), it("uj"), PL, OP.mult), n, r=[k_("uj"), "B"], w=[k_("z")], b=["bB"])
        v(ts(it("zs"), it("z"), 5, OP.arith_shift_right), n, r=[k_("z")], w=[k_("zs")])
        v(tt(it("y"), it("zs"), PY, OP.add), n, r=[k_("zs"), "B"], w=[k_("y")], b=["bB"])
        ms_, fz = T.msk[:, 0:128], T["fz" + hh]
        v(lambda: g.vector.tensor_tensor_scan(ft("sc"), ms_, XF, 0.0, OP.mult, OP.add), n, r=["A", "msk"], w=[k_("sc")], b=["bA"])
        v(ts(fz[:, 0::16], T.ftmp[:, FTMP.index("sc") * 256 + 128 * h + 15:FTMP.index("sc") * 256 + 128 * h + 128:16], 0.0, OP.is_ge, GATE, OP.mult), 8,
          r=[k_("sc"), "fz0" + hh], w=[k_("fz")])
        v(lambda: g.vector.tensor_tensor_scan(fl[:], ms_, fz[:], 0.0, OP.mult, OP.add), n, 0.5, r=["msk", k_("fz")], w=[k_("fl") + "a"])
        FL = [k_("fl") + "a"]
        mm([MM(D[:, 256:384], T.ib[:], T[e][:, 0:128], True, False), MM(D[:, 256:384], T.nib[:], cb("mi", t, h), False, True)], 256,
           r=[e, mi, "ib", "nib"], w=["Dd"], b=["bD"])
        absd = T["absd" + hh][:]
        s(act(absd, D[:, 256:384], AF.Abs), n, r=["Dd"], w=[k_("absd")], b=["bD"])
        mm([MM(D[:, 384:512], T.ib[:], T[e][:, 0:128], True, False), MM(D[:, 384:512], T.ib[:], cb("mi", t, h), False, False),
            MM(D[:, 384:512], fl[:], T.i1024[:], False, True),
            MM(D[:, 128:256], fl[:], T.im512[:], True, False), MM(D[:, 128:256], T.ib[:], absd, False, True)], 5 * 128,
           r=FL + [e, mi, k_("absd"), "ib", "im512", "i1024"], w=["De"], b=["bD"])
        v(ts(it("t2"), D[:, 384:512], 0.5, OP.mult, 512.25, OP.subtract), n, r=["De"], w=[k_("t2")], b=["bD"])
        v(tt(T[eo][:, 0:128], it("t2"), D[:, 128:256], OP.max), n, r=[k_("t2"), "De"], w=[eo], b=["bD"])
        if t < V - 1:
            if h == 1:
                mm([MM(D[:, 0:8], T.onec[:], T["fl%d" % a][:, 0::16], a == 0, a == 1) for a in range(2)], 128, r=FL + ["fl0a", "onec"], w=["Du"], b=["bD"])
                v(lambda: g.vector.tensor_reduce(T.cnt[:, 0:1], D[:, 0:8], AX.X, OP.add), 8, r=["Du"], w=["cnt"], b=["bD"])
                v(ts(T.acol[:, 0:1], T.cnt[:, 0:1], -1.0, OP.mult), 1, r=["cnt"], w=["ac0"])
                v(ts(T.acol[:, 1:2], T.acol[:, 0:1], 31, OP.bitwise_and), 1, r=["ac0"], w=["ac1"])
                v(ms(T[eo][:, 128:144], 0.0), 16, w=[eo + "A"])
                v(cp(T[eo][:, 128:129], T.acol[:, 1:2]), 1, r=["ac1"], w=[eo + "A"])
            else:
                v(ms(T[eo][:, 128:144], 0.0), 16, w=[eo + "A"])
            d1 = dst(-1)
            en = "e%d%d" % (t + 1, h)
            send("re%d%d" % (t + 1, h), T[en][:], T[eo][:], d1, topo.engines(core, d1)[1:8:2], eo, LAT, en, after=[last_w[eo + "A"]])
        else:
            op("Y", 0.1, [lambda: g.sync.dma_start(T.ye[:, 128 * h:128 * h + 128], T[eo][:, 0:128])], r=[eo], sig=("d_ye%d" % h, 16), lat=2.0)
        pst = cb("lst", t, h)
        v(tt(ft("m3"), it("y"), X3, OP.min), n, r=[k_("y"), "A"], w=[k_("m3")], b=["bA"])
        v(tt(ft("r3"), ft("m3"), PL, OP.max), n, r=[k_("m3"), "B"], w=[k_("r3")], b=["bB"])
        v(tt(E[:, 0:128], qo, X2, OP.min), n, r=["qst%d%d" % (t, h), "A"], w=["bE0"], b=["bA", "bE"])
        v(tt(E[:, 128:256], pst, X1, OP.min), n, r=["lst%d%d" % (t, h), "A"], w=["bE1"], b=["bA", "bE"])
        v(tt(ft("m1"), E[:, 128:256], fl[:], OP.subtract), n, r=FL + ["bE1"], w=[k_("m1")], b=["bE"])
        v(tt(E[:, 0:128], ft("r3"), E[:, 0:128], OP.max), n, r=[k_("r3"), "bE0"], w=["bE0"], b=["bE"])
        v(tt(it("r1"), ft("m1"), E[:, 0:128], OP.max), n, r=[k_("m1"), "bE0"], w=[k_("r1")], b=["bE"])
        nw = it("nw")
        v(ts(nw, it("r1"), 4095, OP.bitwise_and), n, r=[k_("r1")], w=[k_("nw")])
        v(ts(cb("lh", t + 1, h), nw, 2048.0, OP.subtract), n, r=[k_("nw")], w=["lh%d%d" % (t + 1, h)])
        if t + 3 < 5:
            v(ts(cb("lst", t + 3, h), nw, CP, OP.add), n, r=[k_("nw")], w=["lst%d%d" % (t + 3, h)])
        qn = cb("qst", t + 1, h)
        v(tt(ft("ne"), nw, PL, OP.not_equal), n, r=[k_("nw"), "B"], w=[k_("ne")], b=["bB"])
        v(tt(E[:, 128:256], ft("ne"), PLQ, OP.mult), n, r=[k_("ne"), "B"], w=["bE1"], b=["bB", "bE"])
        v(tt(qn, qo, E[:, 128:256], OP.add), n, r=["qst%d%d" % (t, h), "bE1"], w=["qst%d%d" % (t + 1, h)], b=["bE"])
        mm([MM(E[:, 256:384], cb("lh", t + 1, h), T.i16[:], True, True)], 128, r=["i16", "lh%d%d" % (t + 1, h)], w=["bE2"], b=["bE"])
        if t < V - 1:
            v(ts(cb("u16l", t + 3, h), E[:, 256:384], 2048.0, OP.add), n, r=["bE2"], w=["u16l%d%d" % (t + 3, h)], b=["bE"])
        v(ts(cb("qh", t + 1, h), qn, CQ + 2048.0, OP.subtract), n, r=["qst%d%d" % (t + 1, h)], w=["qh%d%d" % (t + 1, h)])
        mm([MM(E[:, 384:512], cb("qh", t + 1, h), T.i16[:], True, True)], 128, r=["i16", "qh%d%d" % (t + 1, h)], w=["bE3"], b=["bE"])
        if t < V - 1:
            v(ts(cb("u16q", t + 1, h), E[:, 384:512], 2048.0, OP.add), n, r=["bE3"], w=["u16q%d%d" % (t + 1, h)], b=["bE"])
        if t >= 2:
            o_ = cb("outs", t - 2, h)
            nm = ("yp", "ys", "yl")[t - 2]
            s(act(o_, E[:, 256:384], AF.Copy, 2048.0), n, r=["bE2"], w=["outs%d%d" % (t - 2, h)], b=["bE"])
            op("Y", 0.1, [lambda: g.sync.dma_start(T[nm][:, 128 * h:128 * h + 128], o_)], r=["outs%d%d" % (t - 2, h)], sig=("d_%s%d" % (nm, h), 16), lat=2.0)
        if t == V - 1:
            oq = cb("outs", 3, h)
            s(act(oq, E[:, 384:512], AF.Copy, 2048.0), n, r=["bE3"], w=["outs3%d" % h], b=["bE"])
            op("Y", 0.1, [lambda: g.sync.dma_start(T.yq[:, 128 * h:128 * h + 128], oq)], r=["outs3%d" % h], sig=("d_yq%d" % h, 16), lat=2.0)

    for t in range(V):
        if t < 4:
            tabs(t)
        for h in range(H2):
            big(t, h)
            logic(t, h)
        if t == 1:
            send_table(2, [])
        if t == 2:
            send_table(3, [first[(0, 1)]])
    return ops


def _order(ops):
    n = len(ops)
    pred = [sorted(o["d"]) for o in ops]
    succ = [[] for _ in range(n)]
    for i in range(n):
        for d in pred[i]:
            succ[d].append(i)
    q, c, lat = [o["q"] for o in ops], [o["c"] for o in ops], [o["lat"] for o in ops]

    def list_pass(before, after, prio, forward):
        left = [len(b) for b in before]
        ready_t = [0.0 if forward or after[i] else lat[i] for i in range(n)]
        start, free, ready, seq = [0.0] * n, {}, {}, []
        for i in range(n):
            if not left[i]:
                ready.setdefault(q[i], []).append(i)
        while len(seq) < n:
            best = None
            for qq, lst in ready.items():
                f = free.get(qq, 0.0)
                for i in lst:
                    key = (max(f, ready_t[i]), -prio[i], i)
                    if best is None or key < best:
                        best = key
            st, _, i = best
            ready[q[i]].remove(i)
            seq.append(i)
            start[i] = st
            fin = st + c[i]
            if q[i] != "R":
                free[q[i]] = fin
            for k in after[i]:
                ready_t[k] = max(ready_t[k], fin + lat[i if forward else k] + WAKE)
                left[k] -= 1
                if not left[k]:
                    ready.setdefault(q[k], []).append(k)
        return start, seq

    base = [0.0] * n
    for i in reversed(range(n)):
        base[i] = max([base[k] for k in succ[i]] + [0.0]) + c[i] + lat[i] + WAKE
    rs = np.random.RandomState(SEED)
    best = None
    for trial in range(TRIES):
        prio = [float(p + (SPREAD * x if trial else 0.0)) for p, x in zip(base, rs.random_sample(n))]
        for turn in range(TURNS):
            start, seq = list_pass(pred, succ, prio, True)
            span = max(start[i] + c[i] + lat[i] for i in range(n))
            if best is None or span < best[0] - 1e-9:
                best = (span, start, seq)
            back, _ = list_pass(succ, pred, [start[i] + c[i] for i in range(n)], False)
            prio = [back[i] + c[i] for i in range(n)]
    order = {}
    for i in best[2]:
        ops[i]["st"] = best[1][i]
        order.setdefault(q[i], []).append(ops[i])
    return order


def rank_program(g, core, T, topo):
    if T.rank_of(core) is None:
        return
    ops = _plan(g, core, T, topo)
    order = _order(ops)
    qs = {"T": g.tensor, "V": g.vector, "S": g.scalar, "G": g, "Y": g.sync}
    qsem = {"T": "sT", "V": "sV", "S": "sS", "G": "sG"}
    count = {q: 0 for q in qs}
    known = {q: {} for q in qs}
    sent = 0
    glob = [o for q in order for o in order[q]]
    for q in ("T", "V", "S", "G"):
        c = 0
        for o in order[q]:
            if o["sig"] is None:
                c += len(o["f"])
                o["val"] = (qsem[q], c)
            elif o["sig"][0] == "send":
                o["val"] = None
    for q in ("Y", "R"):
        for o in order[q]:
            o["val"] = o["sig"]
    for o in sorted(glob, key=lambda o: (o["st"], o["i"])):
        o["w"] = []
        if o["q"] == "R":
            o["clk"] = {o["val"][0]: o["val"][1]}
            continue
        kn = known[o["q"]]
        need = {}
        for d in o["d"]:
            x = ops[d]
            if x["val"] is None or (x["q"] == "T" and o["q"] == "T"):
                continue
            sm, vl = x["val"]
            if kn.get(sm, 0) < vl and need.get(sm, (0, None))[0] < vl:
                need[sm] = (vl, x)
        for sm in sorted(need, key=lambda m: -need[m][1]["st"]):
            vl, x = need[sm]
            if kn.get(sm, 0) < vl:
                o["w"].append((sm, vl))
                for a, b in list(x["clk"].items()) + [(sm, vl)]:
                    if kn.get(a, 0) < b:
                        kn[a] = b
        o["clk"] = dict(kn)
        if o["val"] is not None:
            o["clk"][o["val"][0]] = o["val"][1]
    for q in qs:
        eng = qs[q]
        for o in order.get(q, []):
            for sm, vl in o["w"]:
                eng.wait_ge(T.sem[sm], vl)
            for f in o["f"]:
                ins = f()
                if o["sig"] is None:
                    ins.then_inc(T.sem[qsem[q]], 1)
                elif o["sig"][0] == "send":
                    sent += o["sig"][1]
                else:
                    ins.then_inc(T.sem[o["sig"][0]], 16)
    for q in ("T", "V", "S", "G"):
        tot = max([o["val"][1] for o in order[q] if o["val"] is not None] + [0])
        g.sync.wait_ge(T.sem[qsem[q]], tot)
    for nm in STORES:
        g.sync.wait_ge(T.sem["d_" + nm], 16)
    g.wait_ge(T.sem["lsem"], sent)
